import numpy as np
import ml_dtypes


def mxq(x, axis, fmt="e4m3"):
    dtype, down = {"e4m3": (ml_dtypes.float8_e4m3fn, 7), "e5m2": (ml_dtypes.float8_e5m2, 14)}[fmt]
    v = np.moveaxis(np.asarray(x, np.float32).astype(ml_dtypes.bfloat16).astype(np.float64), axis, -1)
    blocks = v.reshape(v.shape[:-1] + (-1, 32))
    amax = np.abs(blocks).max(-1, keepdims=True)
    byte = np.maximum(np.where(amax > 0, np.frexp(amax)[1] - 1 + 127, 0) - down, 1)
    scale = np.exp2(byte - 127.0)
    codes = (blocks / scale).astype(np.float32).astype(dtype).astype(np.float64)
    return np.moveaxis((codes * scale).reshape(v.shape), -1, axis)


WIDE = False


def mx_kscale(k):
    if not WIDE:
        return np.ones(k)
    levels = np.array([24, -24, 12, -12, 0])
    if k % 512:
        return np.exp2(np.random.permutation(np.resize(levels, k // 32))).repeat(32)
    a = np.empty((k // 512, 16))
    for p in range(k // 512):
        a[p, :8] = np.random.permutation(np.resize(levels, 8))
        for g in range(8):
            far = levels[np.abs(levels - a[p, g]) >= 10]
            a[p, g + 8] = far[np.random.randint(len(far))]
    return np.exp2(a.ravel()).repeat(32)


def f64(x):
    return np.asarray(x).astype(np.float64)


E2M1 = np.array([0.0, 0.5, 1.0, 1.5, 2.0, 3.0, 4.0, 6.0, -0.0, -0.5, -1.0, -1.5, -2.0, -3.0, -4.0, -6.0])


def pack_weight(w, fmt):
    k, n = w.shape
    w = f64(np.asarray(w, np.float32).astype(ml_dtypes.bfloat16)).reshape(k // 32, 32, n)
    amax = np.abs(w).max(1)
    if fmt == "e4m3":
        byte = np.frexp(amax)[1] - 1 + 127 - 7
    else:
        mant, ex = np.frexp(amax / 6.0)
        byte = np.where(mant > 0.5, ex, ex - 1) + 127
    byte = np.clip(np.where(amax > 0, byte, 1), 1, 254)
    scaled = (w * np.exp2(127.0 - byte)[:, None, :]).reshape(k, n).astype(np.float32)
    by_word = np.ascontiguousarray(scaled.reshape(k // 512, 128, 4, n).transpose(0, 1, 3, 2))
    if fmt == "e4m3":
        words = by_word.astype(ml_dtypes.float8_e4m3fn).view(np.uint8)
    else:
        c = by_word.astype(ml_dtypes.float4_e2m1fn).view(np.uint8) & 0xF
        words = (c[..., 0::2] | (c[..., 1::2] << 4)).reshape(k // 512, 128, 2 * n)
    return np.ascontiguousarray(words), np.ascontiguousarray(byte.astype(np.uint8).reshape(k // 512, 16, n))


def unpack_weight(words, scales, fmt):
    g, _, n = scales.shape
    words = np.ascontiguousarray(words).reshape(g, 128, n, -1)
    if fmt == "e4m3":
        vals = words.view(ml_dtypes.float8_e4m3fn).astype(np.float64)
    else:
        nib = np.empty((g, 128, n, 4), np.uint8)
        nib[..., 0::2] = words & 0xF
        nib[..., 1::2] = words >> 4
        vals = E2M1[nib]
    vals = vals * np.repeat(np.exp2(scales.astype(np.float64) - 127.0), 8, axis=1)[..., None]
    return vals.transpose(0, 1, 3, 2).reshape(g * 512, n)


def planes(y):
    n, m = y.shape
    v = y.astype(np.float32).astype(ml_dtypes.bfloat16).astype(np.float64).reshape(n // 32, 32, m)
    top = np.abs(v).max(1)
    byte = np.clip(np.where(top > 0, np.frexp(top)[1] - 1 + 127 - 7, 1), 1, 254)
    codes = (v * np.exp2(127.0 - byte)[:, None, :]).reshape(n, m).astype(np.float32).astype(ml_dtypes.float8_e4m3fn).view(np.uint8)
    words = codes.reshape(n // 512, 128, 4, m).transpose(0, 1, 3, 2)
    return np.ascontiguousarray(words), np.ascontiguousarray(byte.astype(np.uint8).reshape(n // 512, 16, m))


def silu(f):
    return f / (1.0 + np.exp(-np.maximum(f, -700.0)))


def gelu(f):
    return 0.5 * f * (1.0 + np.tanh(np.sqrt(2.0 / np.pi) * (f + 0.044715 * f**3)))


K, R, N, T = 1024, 1024, 1024, 512


def setup_inputs():
    n = np.random.standard_normal
    u = mx_kscale(R)[:, None]
    s = mx_kscale(K)[:, None]
    v = n((R, N)) / np.sqrt(R) / u
    p_w4 = pack_weight(n((K, R)) / np.sqrt(K) / s, "e2m1")
    p_v8 = pack_weight(v[:512], "e4m3")
    p_v4 = pack_weight(v[512:], "e2m1")
    return {
        "x": (n((K, T)) * s).astype(np.float32),
        "w4_words": p_w4[0],
        "w4_scales": p_w4[1],
        "sm": (np.random.uniform(0.5, 2.0, R) * u[:, 0]).astype(np.float32),
        "v8_words": p_v8[0],
        "v8_scales": p_v8[1],
        "v4_words": p_v4[0],
        "v4_scales": p_v4[1],
        "b": (0.3 * n(N)).astype(np.float32),
    }


def reference(x, w4_words, w4_scales, sm, v8_words, v8_scales, v4_words, v4_scales, b):
    x_ = mxq(f64(x), 0, "e4m3")
    w4_ = unpack_weight(w4_words, w4_scales, "e2m1")
    a = w4_.T @ x_
    h = f64(sm)[:, None] * silu(a)
    h_ = mxq(h, 0, "e4m3")
    v8_ = unpack_weight(v8_words, v8_scales, "e4m3")
    v4_ = unpack_weight(v4_words, v4_scales, "e2m1")
    y = v8_.T @ h_[:512] + v4_.T @ h_[512:]
    return (gelu(y + f64(b)[:, None]), h) + planes(h)

@@ -1,0 +1,281 @@
+from contextlib import ExitStack
+
+import concourse.mybir as mybir
+
+K, R, N, T = 1024, 1024, 1024, 512
+FLOPS = 2 * K * R * T + 2 * R * N * T
+
+F32 = mybir.dt.float32
+BF16 = mybir.dt.bfloat16
+I32 = mybir.dt.int32
+U32 = mybir.dt.uint32
+U8 = mybir.dt.uint8
+FP8X4 = mybir.dt.float8_e4m3fn_x4
+FP4X4 = mybir.dt.float4_e2m1fn_x4
+ACT = mybir.ActivationFunctionType
+ALU = mybir.AluOpType
+
+P = 128
+PACK = 4
+PASS = P * PACK
+HALF = T // 2
+QUARTER = T // 4
+QUADS = 4
+A4, A8 = 1, 0
+
+X_VEC = 176
+
+
+def tile_mix_save_silu_mix_gelu_kernel(
+    tc, x, w4_words, w4_scales, sm, v8_words, v8_scales, v4_words, v4_scales, b, out_0, out_1, out_2, out_3
+):
+    nc = tc.nc
+    with ExitStack() as ctx:
+        sb = ctx.enter_context(tc.tile_pool(name="sb", bufs=1))
+        ps = ctx.enter_context(tc.psum_pool(name="ps", bufs=1))
+        ctx.enter_context(tc.manual_schedule())
+
+        def tile(name, shape, dtype):
+            return sb.tile(shape, dtype, name=name, align_bytes=64)
+
+        w_raw = [tile("w_raw%d" % a, [P, 2, 2 * PASS], U8) for a in range(2)]
+        w_words = [tile("w_words%d" % a, [P, 2 * PACK * 2 * P], U8) for a in range(2)]
+        ws_raw = tile("ws_raw", [P, 2 * R], U8)
+        w_scale = [tile("w_scale%d" % a, [P, 2 * PACK * P], U8) for a in range(2)]
+        x_raw = [[tile("x_raw%d%d" % (k, h), [P, PACK, HALF], F32) for h in range(2)] for k in range(2)]
+        x_bf = [[tile("x_bf%d%d" % (k, h), [P, HALF * PACK], BF16) for h in range(2)] for k in range(2)]
+        x_words = [tile("x_words%d" % k, [P, T], U32) for k in range(2)]
+        x_scale = [tile("x_scale%d" % k, [P, T], U8) for k in range(2)]
+        sm_sb = tile("sm_sb", [P, 2, PACK], F32)
+        b_sb = tile("b_sb", [P, N // P], F32)
+        zero_in = tile("zero_in", [P, 1], F32)
+        zero = tile("zero", [P, 1], F32)
+        v8_sb = tile("v8_sb", [P, 4 * N], U8)
+        v4_sb = tile("v4_sb", [P, 2 * N], U8)
+        v_scale = tile("v_scale", [P, 2 * N], U8)
+        s_sb = [[tile("s%d%d" % (a, h), [P, PACK, HALF], F32) for h in range(2)] for a in range(2)]
+        h_sb = [[tile("h%d%d" % (a, h), [P, PACK, HALF], F32) for h in range(2)] for a in range(2)]
+        h_bf = [[tile("hb%d%d" % (a, h), [P, HALF * PACK], BF16) for h in range(2)] for a in range(2)]
+        h_words = [tile("h_words%d" % a, [P, T], U32) for a in range(2)]
+        h_scale = tile("h_scale", [P, 2 * T], U8)
+        y_sb = [[tile("y%d%d" % (h, g), [P, 2, HALF], F32) for g in range(4)] for h in range(2)]
+
+        def half(h):
+            return slice(h * HALF, (h + 1) * HALF)
+
+        nc.vector.memset(ws_raw[:].bitcast(I32), 0)
+        nc.vector.memset(zero_in[:], 0.0)
+        nc.vector.memset(v_scale[:].bitcast(I32), 0)
+        nc.scalar.activation(out=zero[:], in_=zero_in[:], func=ACT.Silu)
+
+        def load_w(a):
+            src = w4_words[:, :, a * 2 * PASS : (a + 1) * 2 * PASS].rearrange("k p n -> p k n")
+            nc.sync.dma_start(out=w_raw[a][:].bitcast(I32), in_=src.bitcast(I32))
+
+        def load_scale_rows(dst, src):
+            passes = src.shape[0]
+            for q in range(QUADS):
+                rows = src[:, 4 * q : 4 * q + 4, :].rearrange("k r n -> r k n")
+                nc.sync.dma_start(
+                    out=dst[32 * q : 32 * q + 4, :].bitcast(I32).rearrange("r (k n) -> r k n", k=passes),
+                    in_=rows.bitcast(I32),
+                )
+
+        load_w(A4)
+        load_scale_rows(ws_raw[:], w4_scales)
+        for k in range(2):
+            for h in range(2):
+                rows = x[k * PASS : (k + 1) * PASS, half(h)].rearrange("(p j) t -> p j t", j=PACK)
+                nc.sync.dma_start(out=x_raw[k][h][:], in_=rows)
+        load_w(A8)
+        nc.sync.dma_start(out=sm_sb[:], in_=sm.rearrange("(a p j) -> p a j", a=2, j=PACK))
+        nc.sync.dma_start(out=v4_sb[:].bitcast(I32), in_=v4_words[0].bitcast(I32))
+        load_scale_rows(v_scale[:, N : 2 * N], v4_scales)
+        nc.sync.dma_start(out=v8_sb[:].bitcast(I32), in_=v8_words[0].rearrange("p n i -> p (n i)").bitcast(I32))
+        load_scale_rows(v_scale[:, 0:N], v8_scales)
+        with nc.allow_non_contiguous_dma(reason="one bias value for each partition"):
+            nc.sync.dma_start(out=b_sb[:], in_=b.rearrange("(c p) -> p c", p=P))
+
+        def deal_words(a):
+            nc.vector.tensor_copy(
+                out=w_words[a][:].rearrange("p (k j m e) -> p k j m e", k=2, j=PACK, e=2),
+                in_=w_raw[a][:].rearrange("p k (m j e) -> p k j m e", j=PACK, e=2),
+            )
+
+        def deal_scales(a):
+            cols = ws_raw[:].rearrange("p (k n) -> p k n", k=2)[:, :, a * PASS : (a + 1) * PASS]
+            nc.vector.tensor_copy(
+                out=w_scale[a][:].rearrange("p (k j m) -> p k j m", k=2, j=PACK),
+                in_=cols.rearrange("p k (m j) -> p k j m", j=PACK),
+            )
+
+        def interleave(copy, dst, src, lo, hi):
+            copy(
+                out=dst[:, lo * PACK : hi * PACK].rearrange("p (t j) -> p t j", j=PACK),
+                in_=src[:, :, lo:hi].rearrange("p j t -> p t j"),
+            )
+
+        def quantize(words, scale, src):
+            nc.vector.quantize_mx(out=words.bitcast(FP8X4), scales=scale, in_=src)
+
+        def round_x(k, h):
+            interleave(nc.scalar.copy, x_bf[k][h], x_raw[k][h], X_VEC, HALF)
+            interleave(nc.vector.tensor_copy, x_bf[k][h], x_raw[k][h], 0, X_VEC)
+
+        def quantize_x(k, h):
+            quantize(x_words[k][:, half(h)], x_scale[k][:, half(h)], x_bf[k][h][:])
+
+        deal_words(A4)
+        round_x(0, 0)
+        deal_scales(A4)
+        quantize_x(0, 0)
+        round_x(0, 1)
+        deal_scales(A8)
+        quantize_x(0, 1)
+        round_x(1, 0)
+        round_x(1, 1)
+        quantize_x(1, 0)
+        quantize_x(1, 1)
+        deal_words(A8)
+
+        acc1 = [[ps.tile([P, T], F32, name="acc1_%d%d" % (a, j), tag="bank%d" % (PACK * a + j)) for j in range(PACK)] for a in range(2)]
+
+        def pass1(a, j, k, lo=0, hi=T):
+            c = k * PACK + j
+            nc.tensor.matmul_mx(
+                out=acc1[a][j][:, lo:hi],
+                lhsT=w_words[a][:, c * 2 * P : (c + 1) * 2 * P].bitcast(FP4X4),
+                lhsT_scale=w_scale[a][:, c * P : (c + 1) * P],
+                rhs=x_words[k][:, lo:hi].bitcast(FP8X4),
+                rhs_scale=x_scale[k][:, lo:hi],
+                start=(k == 0 and lo == 0),
+                stop=(k == 1),
+            )
+
+        for h in range(2):
+            for j in range(PACK):
+                for lo in range(h * HALF, (h + 1) * HALF, QUARTER):
+                    pass1(A4, j, 0, lo, lo + QUARTER)
+        for j in range(PACK):
+            pass1(A4, j, 1)
+        for j in range(PACK):
+            for k in range(2):
+                pass1(A8, j, k)
+
+        def silu(a, h):
+            for j in range(PACK):
+                nc.scalar.activation(out=s_sb[a][h][:, j, :], in_=acc1[a][j][:, half(h)], func=ACT.Silu, bias=zero[:])
+
+        def smooth(a, h, js):
+            for j in js:
+                nc.vector.tensor_scalar(
+                    out=h_sb[a][h][:, j, :], in0=s_sb[a][h][:, j, :], scalar1=sm_sb[:, a, j : j + 1], scalar2=None, op0=ALU.mult
+                )
+
+        def store_h(a, h):
+            rows = out_1[a * PASS : (a + 1) * PASS, half(h)].rearrange("(p j) t -> p j t", j=PACK)
+            nc.sync.dma_start(out=rows, in_=h_sb[a][h][:])
+
+        def round_h(a, h):
+            interleave(nc.vector.tensor_copy, h_bf[a][h], h_sb[a][h], 0, HALF)
+
+        def h_scale_cols(a, lo, hi):
+            return h_scale[:, a * T + lo : a * T + hi]
+
+        def quantize_h(a, h):
+            quantize(h_words[a][:, half(h)], h_scale_cols(a, h * HALF, (h + 1) * HALF), h_bf[a][h][:])
+
+        def store_words(a):
+            nc.sync.dma_start(out=out_2[a].rearrange("p t i -> p (t i)").bitcast(I32), in_=h_words[a][:].bitcast(I32))
+
+        for a in (A4, A8):
+            for h in range(2):
+                silu(a, h)
+
+        smooth(A4, 0, range(PACK))
+        store_h(A4, 0)
+        smooth(A4, 1, range(1))
+        round_h(A4, 0)
+        smooth(A4, 1, range(1, PACK))
+        store_h(A4, 1)
+        quantize_h(A4, 0)
+        round_h(A4, 1)
+        smooth(A8, 0, range(PACK))
+        store_h(A8, 0)
+        quantize_h(A4, 1)
+        store_words(A4)
+        round_h(A8, 0)
+        smooth(A8, 1, range(PACK))
+        store_h(A8, 1)
+        quantize_h(A8, 0)
+        round_h(A8, 1)
+        quantize_h(A8, 1)
+
+        acc2 = [
+            [ps.tile([P, 2, HALF], F32, name="acc2_%d%d" % (h, g), tag="bank%d" % (PACK * (A4, A8)[h] + g)) for g in range(4)]
+            for h in range(2)
+        ]
+
+        def pass_v4(h, g):
+            for u in range(2):
+                c = 2 * g + u
+                for q in range(2):
+                    lo = h * HALF + q * QUARTER
+                    nc.tensor.matmul_mx(
+                        out=acc2[h][g][:, u, q * QUARTER : (q + 1) * QUARTER],
+                        lhsT=v4_sb[:, c * 2 * P : (c + 1) * 2 * P].bitcast(FP4X4),
+                        lhsT_scale=v_scale[:, N + c * P : N + (c + 1) * P],
+                        rhs=h_words[A4][:, lo : lo + QUARTER].bitcast(FP8X4),
+                        rhs_scale=h_scale_cols(A4, lo, lo + QUARTER),
+                        start=(u == 0 and q == 0),
+                        stop=False,
+                    )
+
+        def pass_v8(h, g):
+            for u in range(2):
+                c = 2 * g + u
+                nc.tensor.matmul_mx(
+                    out=acc2[h][g][:, u, :],
+                    lhsT=v8_sb[:, c * 4 * P : (c + 1) * 4 * P].bitcast(FP8X4),
+                    lhsT_scale=v_scale[:, c * P : (c + 1) * P],
+                    rhs=h_words[A8][:, half(h)].bitcast(FP8X4),
+                    rhs_scale=h_scale_cols(A8, h * HALF, (h + 1) * HALF),
+                    start=False,
+                    stop=(u == 1),
+                )
+
+        def gelu(h, g, last=False):
+            for u in range(2):
+                c = 2 * g + u
+                nc.scalar.activation(
+                    out=y_sb[h][g][:, u, :], in_=acc2[h][g][:, u, :], func=ACT.Gelu_apprx_tanh, bias=b_sb[:, c : c + 1]
+                )
+                if last:
+                    nc.sync.dma_start(out=out_0[c * P : (c + 1) * P, half(h)], in_=y_sb[h][g][:, u, :])
+            if not last:
+                rows = out_0[2 * g * P : (2 * g + 2) * P, half(h)].rearrange("(u p) t -> p u t", p=P)
+                nc.sync.dma_start(out=rows, in_=y_sb[h][g][:])
+
+        for g in range(4):
+            pass_v4(0, g)
+        for g in range(2):
+            pass_v4(1, g)
+        for g in range(4):
+            pass_v8(0, g)
+        for g in range(2, 4):
+            pass_v4(1, g)
+        for g in range(4):
+            pass_v8(1, g)
+
+        gelu(0, 0)
+        store_words(A8)
+        for q in range(QUADS):
+            rows = out_3[:, 4 * q : 4 * q + 4, :].rearrange("a r t -> r a t")
+            nc.sync.dma_start(
+                out=rows.bitcast(I32),
+                in_=h_scale[32 * q : 32 * q + 4, :].bitcast(I32).rearrange("r (a t) -> r a t", a=2),
+            )
+        for g in range(1, 4):
+            gelu(0, g)
+        for g in range(4):
+            gelu(1, g, last=(g == 3))

@@ -21,9 +21,12 @@ PASS = P * PACK
 HALF = T // 2
 QUARTER = T // 4
 QUADS = 4
+SQ = 32
+TILES = N // P
+RUN = 4
 A4, A8 = 1, 0
 
-X_VEC = 176
+X_VEC = 320
 
 
 def tile_mix_save_silu_mix_gelu_kernel(
@@ -42,29 +45,32 @@ def tile_mix_save_silu_mix_gelu_kernel(
         w_words = [tile("w_words%d" % a, [P, 2 * PACK * 2 * P], U8) for a in range(2)]
         ws_raw = tile("ws_raw", [P, 2 * R], U8)
         w_scale = [tile("w_scale%d" % a, [P, 2 * PACK * P], U8) for a in range(2)]
-        x_raw = [[tile("x_raw%d%d" % (k, h), [P, PACK, HALF], F32) for h in range(2)] for k in range(2)]
-        x_bf = [[tile("x_bf%d%d" % (k, h), [P, HALF * PACK], BF16) for h in range(2)] for k in range(2)]
+        x_raw = [tile("x_raw%d" % k, [P, PACK, T], F32) for k in range(2)]
+        x_bf = [tile("x_bf%d" % k, [P, T * PACK], BF16) for k in range(2)]
         x_words = [tile("x_words%d" % k, [P, T], U32) for k in range(2)]
         x_scale = [tile("x_scale%d" % k, [P, T], U8) for k in range(2)]
-        sm_sb = tile("sm_sb", [P, 2, PACK], F32)
-        b_sb = tile("b_sb", [P, N // P], F32)
+        sm_sb = tile("sm_sb", [P, 2, 2 * PACK], F32)
+        b_rows = tile("b_rows", [P, TILES * SQ], F32)
+        b_cols = tile("b_cols", [P, TILES * SQ], F32)
         zero_in = tile("zero_in", [P, 1], F32)
         zero = tile("zero", [P, 1], F32)
+
         v8_sb = tile("v8_sb", [P, 4 * N], U8)
         v4_sb = tile("v4_sb", [P, 2 * N], U8)
         v_scale = tile("v_scale", [P, 2 * N], U8)
         s_sb = [[tile("s%d%d" % (a, h), [P, PACK, HALF], F32) for h in range(2)] for a in range(2)]
-        h_sb = [[tile("h%d%d" % (a, h), [P, PACK, HALF], F32) for h in range(2)] for a in range(2)]
-        h_bf = [[tile("hb%d%d" % (a, h), [P, HALF * PACK], BF16) for h in range(2)] for a in range(2)]
+        h_sb = [tile("h%d" % a, [P, PACK, T], F32) for a in range(2)]
+        h_bf = [tile("hb%d" % a, [P, T * PACK], BF16) for a in range(2)]
         h_words = [tile("h_words%d" % a, [P, T], U32) for a in range(2)]
         h_scale = tile("h_scale", [P, 2 * T], U8)
-        y_sb = [[tile("y%d%d" % (h, g), [P, 2, HALF], F32) for g in range(4)] for h in range(2)]
+        y_sb = [tile("y%d" % c, [P, T], F32) for c in range(TILES)]
 
         def half(h):
             return slice(h * HALF, (h + 1) * HALF)
 
         nc.vector.memset(ws_raw[:].bitcast(I32), 0)
         nc.vector.memset(zero_in[:], 0.0)
+        nc.vector.memset(b_rows[:], 0.0)
         nc.vector.memset(v_scale[:].bitcast(I32), 0)
         nc.scalar.activation(out=zero[:], in_=zero_in[:], func=ACT.Silu)
 
@@ -84,17 +90,16 @@ def tile_mix_save_silu_mix_gelu_kernel(
         load_w(A4)
         load_scale_rows(ws_raw[:], w4_scales)
         for k in range(2):
-            for h in range(2):
-                rows = x[k * PASS : (k + 1) * PASS, half(h)].rearrange("(p j) t -> p j t", j=PACK)
-                nc.sync.dma_start(out=x_raw[k][h][:], in_=rows)
+            nc.sync.dma_start(out=x_raw[k][:], in_=x[k * PASS : (k + 1) * PASS, :].rearrange("(p j) t -> p j t", j=PACK))
+        nc.scalar.dma_start(
+            out=b_rows[0:P:SQ, :].rearrange("q (c i) -> q c i", i=SQ), in_=b.rearrange("(c q i) -> q c i", q=QUADS, i=SQ)
+        )
+        nc.scalar.dma_start(out=sm_sb[:, :, 0:PACK], in_=sm.rearrange("(a p j) -> p a j", a=2, j=PACK))
         load_w(A8)
-        nc.sync.dma_start(out=sm_sb[:], in_=sm.rearrange("(a p j) -> p a j", a=2, j=PACK))
         nc.sync.dma_start(out=v4_sb[:].bitcast(I32), in_=v4_words[0].bitcast(I32))
         load_scale_rows(v_scale[:, N : 2 * N], v4_scales)
         nc.sync.dma_start(out=v8_sb[:].bitcast(I32), in_=v8_words[0].rearrange("p n i -> p (n i)").bitcast(I32))
         load_scale_rows(v_scale[:, 0:N], v8_scales)
-        with nc.allow_non_contiguous_dma(reason="one bias value for each partition"):
-            nc.sync.dma_start(out=b_sb[:], in_=b.rearrange("(c p) -> p c", p=P))
 
         def deal_words(a):
             nc.vector.tensor_copy(
@@ -109,165 +114,112 @@ def tile_mix_save_silu_mix_gelu_kernel(
                 in_=cols.rearrange("p k (m j) -> p k j m", j=PACK),
             )
 
-        def interleave(copy, dst, src, lo, hi):
+        def interleave(copy, dst, src):
             copy(
-                out=dst[:, lo * PACK : hi * PACK].rearrange("p (t j) -> p t j", j=PACK),
-                in_=src[:, :, lo:hi].rearrange("p j t -> p t j"),
+                out=dst.rearrange("p (c i j) -> p c j i", i=RUN, j=PACK),
+                in_=src.rearrange("p j (c i) -> p c j i", i=RUN),
             )
+
+        def round_x(copy, k, lo, hi):
+            interleave(copy, x_bf[k][:, lo * PACK : hi * PACK], x_raw[k][:, :, lo:hi])
 
         def quantize(words, scale, src):
             nc.vector.quantize_mx(out=words.bitcast(FP8X4), scales=scale, in_=src)
 
-        def round_x(k, h):
-            interleave(nc.scalar.copy, x_bf[k][h], x_raw[k][h], X_VEC, HALF)
-            interleave(nc.vector.tensor_copy, x_bf[k][h], x_raw[k][h], 0, X_VEC)
-
-        def quantize_x(k, h):
-            quantize(x_words[k][:, half(h)], x_scale[k][:, half(h)], x_bf[k][h][:])
+        def prepare_x(k):
+            round_x(nc.scalar.copy, k, X_VEC, T)
+            round_x(nc.vector.tensor_copy, k, 0, HALF)
+            round_x(nc.vector.tensor_copy, k, HALF, X_VEC)
+            for h in range(2):
+                quantize(x_words[k][:, half(h)], x_scale[k][:, half(h)], x_bf[k][:, h * HALF * PACK : (h + 1) * HALF * PACK])
 
         deal_words(A4)
-        round_x(0, 0)
         deal_scales(A4)
-        quantize_x(0, 0)
-        round_x(0, 1)
         deal_scales(A8)
-        quantize_x(0, 1)
-        round_x(1, 0)
-        round_x(1, 1)
-        quantize_x(1, 0)
-        quantize_x(1, 1)
+        nc.vector.transpose(out=b_cols[:], in_=b_rows[:])
+        prepare_x(0)
+        prepare_x(1)
         deal_words(A8)
 
         acc1 = [[ps.tile([P, T], F32, name="acc1_%d%d" % (a, j), tag="bank%d" % (PACK * a + j)) for j in range(PACK)] for a in range(2)]
 
-        def pass1(a, j, k, lo=0, hi=T):
+        def pass1(a, j, k):
             c = k * PACK + j
             nc.tensor.matmul_mx(
-                out=acc1[a][j][:, lo:hi],
+                out=acc1[a][j][:],
                 lhsT=w_words[a][:, c * 2 * P : (c + 1) * 2 * P].bitcast(FP4X4),
                 lhsT_scale=w_scale[a][:, c * P : (c + 1) * P],
-                rhs=x_words[k][:, lo:hi].bitcast(FP8X4),
-                rhs_scale=x_scale[k][:, lo:hi],
-                start=(k == 0 and lo == 0),
+                rhs=x_words[k][:].bitcast(FP8X4),
+                rhs_scale=x_scale[k][:],
+                start=(k == 0),
                 stop=(k == 1),
             )
 
-        for h in range(2):
+        for k in range(2):
             for j in range(PACK):
-                for lo in range(h * HALF, (h + 1) * HALF, QUARTER):
-                    pass1(A4, j, 0, lo, lo + QUARTER)
-        for j in range(PACK):
-            pass1(A4, j, 1)
+                pass1(A4, j, k)
         for j in range(PACK):
             for k in range(2):
                 pass1(A8, j, k)
 
-        def silu(a, h):
-            for j in range(PACK):
+        def silu(a, h, js):
+            for j in js:
                 nc.scalar.activation(out=s_sb[a][h][:, j, :], in_=acc1[a][j][:, half(h)], func=ACT.Silu, bias=zero[:])
 
         def smooth(a, h, js):
             for j in js:
                 nc.vector.tensor_scalar(
-                    out=h_sb[a][h][:, j, :], in0=s_sb[a][h][:, j, :], scalar1=sm_sb[:, a, j : j + 1], scalar2=None, op0=ALU.mult
+                    out=h_sb[a][:, j, half(h)], in0=s_sb[a][h][:, j, :], scalar1=sm_sb[:, a, j : j + 1], scalar2=None, op0=ALU.mult
                 )
 
-        def store_h(a, h):
-            rows = out_1[a * PASS : (a + 1) * PASS, half(h)].rearrange("(p j) t -> p j t", j=PACK)
-            nc.sync.dma_start(out=rows, in_=h_sb[a][h][:])
+        def smooth_on_scalar(a, h, js):
+            for j in js:
+                nc.scalar.activation(out=h_sb[a][:, j, half(h)], in_=s_sb[a][h][:, j, :], func=ACT.Copy, scale=sm_sb[:, a, j : j + 1])
 
-        def round_h(a, h):
-            interleave(nc.vector.tensor_copy, h_bf[a][h], h_sb[a][h], 0, HALF)
+        def store_h(a, lo, hi):
+            rows = out_1[a * PASS : (a + 1) * PASS, :].rearrange("(p j) t -> p j t", j=PACK)
+            nc.sync.dma_start(out=rows[:, lo:hi, :], in_=h_sb[a][:, lo:hi, :])
 
-        def h_scale_cols(a, lo, hi):
-            return h_scale[:, a * T + lo : a * T + hi]
+        def round_h(a, cols):
+            interleave(nc.vector.tensor_copy, h_bf[a][:, cols.start * PACK : cols.stop * PACK], h_sb[a][:, :, cols])
 
-        def quantize_h(a, h):
-            quantize(h_words[a][:, half(h)], h_scale_cols(a, h * HALF, (h + 1) * HALF), h_bf[a][h][:])
+        def h_scale_cols(a, cols):
+            return h_scale[:, a * T + cols.start : a * T + cols.stop]
+
+        def quantize_h(a, cols):
+            quantize(h_words[a][:, cols], h_scale_cols(a, cols), h_bf[a][:, cols.start * PACK : cols.stop * PACK])
 
         def store_words(a):
             nc.sync.dma_start(out=out_2[a].rearrange("p t i -> p (t i)").bitcast(I32), in_=h_words[a][:].bitcast(I32))
 
         for a in (A4, A8):
             for h in range(2):
-                silu(a, h)
+                silu(a, h, range(PACK))
 
         smooth(A4, 0, range(PACK))
-        store_h(A4, 0)
         smooth(A4, 1, range(1))
-        round_h(A4, 0)
-        smooth(A4, 1, range(1, PACK))
-        store_h(A4, 1)
-        quantize_h(A4, 0)
-        round_h(A4, 1)
-        smooth(A8, 0, range(PACK))
-        store_h(A8, 0)
-        quantize_h(A4, 1)
+        store_h(A4, 0, 1)
+        round_h(A4, half(0))
+        for j in range(1, PACK):
+            smooth(A4, 1, range(j, j + 1))
+            store_h(A4, j, j + 1)
+        quantize_h(A4, half(0))
+        round_h(A4, half(1))
+        smooth(A8, 0, range(1))
+        quantize_h(A4, half(1))
         store_words(A4)
-        round_h(A8, 0)
-        smooth(A8, 1, range(PACK))
-        store_h(A8, 1)
-        quantize_h(A8, 0)
-        round_h(A8, 1)
-        quantize_h(A8, 1)
-
-        acc2 = [
-            [ps.tile([P, 2, HALF], F32, name="acc2_%d%d" % (h, g), tag="bank%d" % (PACK * (A4, A8)[h] + g)) for g in range(4)]
-            for h in range(2)
-        ]
-
-        def pass_v4(h, g):
-            for u in range(2):
-                c = 2 * g + u
-                for q in range(2):
-                    lo = h * HALF + q * QUARTER
-                    nc.tensor.matmul_mx(
-                        out=acc2[h][g][:, u, q * QUARTER : (q + 1) * QUARTER],
-                        lhsT=v4_sb[:, c * 2 * P : (c + 1) * 2 * P].bitcast(FP4X4),
-                        lhsT_scale=v_scale[:, N + c * P : N + (c + 1) * P],
-                        rhs=h_words[A4][:, lo : lo + QUARTER].bitcast(FP8X4),
-                        rhs_scale=h_scale_cols(A4, lo, lo + QUARTER),
-                        start=(u == 0 and q == 0),
-                        stop=False,
-                    )
-
-        def pass_v8(h, g):
-            for u in range(2):
-                c = 2 * g + u
-                nc.tensor.matmul_mx(
-                    out=acc2[h][g][:, u, :],
-                    lhsT=v8_sb[:, c * 4 * P : (c + 1) * 4 * P].bitcast(FP8X4),
-                    lhsT_scale=v_scale[:, c * P : (c + 1) * P],
-                    rhs=h_words[A8][:, half(h)].bitcast(FP8X4),
-                    rhs_scale=h_scale_cols(A8, h * HALF, (h + 1) * HALF),
-                    start=False,
-                    stop=(u == 1),
-                )
-
-        def gelu(h, g, last=False):
-            for u in range(2):
-                c = 2 * g + u
-                nc.scalar.activation(
-                    out=y_sb[h][g][:, u, :], in_=acc2[h][g][:, u, :], func=ACT.Gelu_apprx_tanh, bias=b_sb[:, c : c + 1]
-                )
-                if last:
-                    nc.sync.dma_start(out=out_0[c * P : (c + 1) * P, half(h)], in_=y_sb[h][g][:, u, :])
-            if not last:
-                rows = out_0[2 * g * P : (2 * g + 2) * P, half(h)].rearrange("(u p) t -> p u t", p=P)
-                nc.sync.dma_start(out=rows, in_=y_sb[h][g][:])
-
-        for g in range(4):
-            pass_v4(0, g)
-        for g in range(2):
-            pass_v4(1, g)
-        for g in range(4):
-            pass_v8(0, g)
-        for g in range(2, 4):
-            pass_v4(1, g)
-        for g in range(4):
-            pass_v8(1, g)
-
-        gelu(0, 0)
+        smooth(A8, 0, range(1, PACK))
+        round_h(A8, half(0))
+        smooth(A8, 1, range(1))
+        smooth_on_scalar(A8, 1, range(1, PACK))
+        store_h(A8, 0, 2)
+        store_h(A8, 2, 4)
+        quantize_h(A8, half(0))
+        quarters = [slice(lo, lo + QUARTER) for lo in range(HALF, T, QUARTER)]
+        for cols in quarters:
+            round_h(A8, cols)
+        for cols in quarters:
+            quantize_h(A8, cols)
         store_words(A8)
         for q in range(QUADS):
             rows = out_3[:, 4 * q : 4 * q + 4, :].rearrange("a r t -> r a t")
@@ -275,7 +227,44 @@ def tile_mix_save_silu_mix_gelu_kernel(
                 out=rows.bitcast(I32),
                 in_=h_scale[32 * q : 32 * q + 4, :].bitcast(I32).rearrange("r (a t) -> r a t", a=2),
             )
-        for g in range(1, 4):
-            gelu(0, g)
-        for g in range(4):
-            gelu(1, g, last=(g == 3))
+
+
+        acc2 = [ps.tile([P, T], F32, name="acc2_%d" % c, tag="bank%d" % ((PACK * A4 + c) % TILES)) for c in range(TILES)]
+
+        def pass_v4(c):
+            nc.tensor.matmul_mx(
+                out=acc2[c][:],
+                lhsT=v4_sb[:, c * 2 * P : (c + 1) * 2 * P].bitcast(FP4X4),
+                lhsT_scale=v_scale[:, N + c * P : N + (c + 1) * P],
+                rhs=h_words[A4][:].bitcast(FP8X4),
+                rhs_scale=h_scale_cols(A4, slice(0, T)),
+                start=True,
+                stop=False,
+            )
+
+        def pass_v8(c, cols):
+            nc.tensor.matmul_mx(
+                out=acc2[c][:, cols],
+                lhsT=v8_sb[:, c * 4 * P : (c + 1) * 4 * P].bitcast(FP8X4),
+                lhsT_scale=v_scale[:, c * P : (c + 1) * P],
+                rhs=h_words[A8][:, cols].bitcast(FP8X4),
+                rhs_scale=h_scale_cols(A8, cols),
+                start=False,
+                stop=(cols.stop == T),
+            )
+
+        for c in range(PACK + 1):
+            pass_v4(c)
+        for c in range(PACK):
+            pass_v8(c, half(0))
+        pass_v4(PACK + 1)
+        for c in range(PACK):
+            pass_v8(c, half(1))
+        for c in range(PACK, TILES):
+            if c > PACK + 1:
+                pass_v4(c)
+            pass_v8(c, slice(0, T))
+
+        for c in range(TILES):
+            nc.scalar.activation(out=y_sb[c][:], in_=acc2[c][:], func=ACT.Gelu_apprx_tanh, bias=b_cols[:, c * SQ : c * SQ + 1])
+            nc.sync.dma_start(out=out_0[c * P : (c + 1) * P, :], in_=y_sb[c][:])

@@ -19,13 +19,13 @@ P = 128
 PACK = 4
 PASS = P * PACK
 HALF = T // 2
-QUARTER = T // 4
 QUADS = 4
 SQ = 32
 TILES = N // P
 RUN = 4
 A4, A8 = 1, 0
 
+H_VEC = 368
 X_VEC = 320
 
 
@@ -58,7 +58,7 @@ def tile_mix_save_silu_mix_gelu_kernel(
         v8_sb = tile("v8_sb", [P, 4 * N], U8)
         v4_sb = tile("v4_sb", [P, 2 * N], U8)
         v_scale = tile("v_scale", [P, 2 * N], U8)
-        s_sb = [[tile("s%d%d" % (a, h), [P, PACK, HALF], F32) for h in range(2)] for a in range(2)]
+        s_sb = [[tile("s%d%d" % (a, j), [P, T], F32) for j in range(PACK)] for a in range(2)]
         h_sb = [tile("h%d" % a, [P, PACK, T], F32) for a in range(2)]
         h_bf = [tile("hb%d" % a, [P, T * PACK], BF16) for a in range(2)]
         h_words = [tile("h_words%d" % a, [P, T], U32) for a in range(2)]
@@ -162,26 +162,20 @@ def tile_mix_save_silu_mix_gelu_kernel(
             for k in range(2):
                 pass1(A8, j, k)
 
-        def silu(a, h, js):
-            for j in js:
-                nc.scalar.activation(out=s_sb[a][h][:, j, :], in_=acc1[a][j][:, half(h)], func=ACT.Silu, bias=zero[:])
+        def silu(a, j, cols):
+            nc.scalar.activation(out=s_sb[a][j][:, cols], in_=acc1[a][j][:, cols], func=ACT.Silu, bias=zero[:])
 
-        def smooth(a, h, js):
-            for j in js:
-                nc.vector.tensor_scalar(
-                    out=h_sb[a][:, j, half(h)], in0=s_sb[a][h][:, j, :], scalar1=sm_sb[:, a, j : j + 1], scalar2=None, op0=ALU.mult
-                )
-
-        def smooth_on_scalar(a, h, js):
-            for j in js:
-                nc.scalar.activation(out=h_sb[a][:, j, half(h)], in_=s_sb[a][h][:, j, :], func=ACT.Copy, scale=sm_sb[:, a, j : j + 1])
+        def smooth(a, j, cols):
+            nc.vector.tensor_scalar(
+                out=h_sb[a][:, j, cols], in0=s_sb[a][j][:, cols], scalar1=sm_sb[:, a, j : j + 1], scalar2=None, op0=ALU.mult
+            )
 
         def store_h(a, lo, hi):
             rows = out_1[a * PASS : (a + 1) * PASS, :].rearrange("(p j) t -> p j t", j=PACK)
             nc.sync.dma_start(out=rows[:, lo:hi, :], in_=h_sb[a][:, lo:hi, :])
 
-        def round_h(a, cols):
-            interleave(nc.vector.tensor_copy, h_bf[a][:, cols.start * PACK : cols.stop * PACK], h_sb[a][:, :, cols])
+        def round_h(copy, a, cols):
+            interleave(copy, h_bf[a][:, cols.start * PACK : cols.stop * PACK], h_sb[a][:, :, cols])
 
         def h_scale_cols(a, cols):
             return h_scale[:, a * T + cols.start : a * T + cols.stop]
@@ -192,34 +186,36 @@ def tile_mix_save_silu_mix_gelu_kernel(
         def store_words(a):
             nc.sync.dma_start(out=out_2[a].rearrange("p t i -> p (t i)").bitcast(I32), in_=h_words[a][:].bitcast(I32))
 
+        whole = slice(0, T)
+        last = PACK - 1
         for a in (A4, A8):
-            for h in range(2):
-                silu(a, h, range(PACK))
+            for j in range(PACK):
+                silu(a, j, whole)
 
-        smooth(A4, 0, range(PACK))
-        smooth(A4, 1, range(1))
-        store_h(A4, 0, 1)
-        round_h(A4, half(0))
-        for j in range(1, PACK):
-            smooth(A4, 1, range(j, j + 1))
+        for j in range(last):
+            smooth(A4, j, whole)
             store_h(A4, j, j + 1)
+        for h in range(2):
+            smooth(A4, last, half(h))
+        store_h(A4, last, PACK)
+        round_h(nc.vector.tensor_copy, A4, half(0))
+        smooth(A8, 0, whole)
+        store_h(A8, 0, 1)
         quantize_h(A4, half(0))
-        round_h(A4, half(1))
-        smooth(A8, 0, range(1))
+        smooth(A8, 1, whole)
+        store_h(A8, 1, 2)
+        round_h(nc.vector.tensor_copy, A4, half(1))
+        smooth(A8, 2, whole)
+        store_h(A8, 2, last)
+        nc.scalar.activation(out=h_sb[A8][:, last, :], in_=s_sb[A8][last][:], func=ACT.Copy, scale=sm_sb[:, A8, last : last + 1])
+        store_h(A8, last, PACK)
         quantize_h(A4, half(1))
         store_words(A4)
-        smooth(A8, 0, range(1, PACK))
-        round_h(A8, half(0))
-        smooth(A8, 1, range(1))
-        smooth_on_scalar(A8, 1, range(1, PACK))
-        store_h(A8, 0, 2)
-        store_h(A8, 2, 4)
-        quantize_h(A8, half(0))
-        quarters = [slice(lo, lo + QUARTER) for lo in range(HALF, T, QUARTER)]
-        for cols in quarters:
-            round_h(A8, cols)
-        for cols in quarters:
-            quantize_h(A8, cols)
+        round_h(nc.scalar.copy, A8, slice(H_VEC, T))
+        round_h(nc.vector.tensor_copy, A8, half(0))
+        round_h(nc.vector.tensor_copy, A8, slice(HALF, H_VEC))
+        for h in range(2):
+            quantize_h(A8, half(h))
         store_words(A8)
         for q in range(QUADS):
             rows = out_3[:, 4 * q : 4 * q + 4, :].rearrange("a r t -> r a t")
@@ -231,14 +227,14 @@ def tile_mix_save_silu_mix_gelu_kernel(
 
         acc2 = [ps.tile([P, T], F32, name="acc2_%d" % c, tag="bank%d" % ((PACK * A4 + c) % TILES)) for c in range(TILES)]
 
-        def pass_v4(c):
+        def pass_v4(c, cols):
             nc.tensor.matmul_mx(
-                out=acc2[c][:],
+                out=acc2[c][:, cols],
                 lhsT=v4_sb[:, c * 2 * P : (c + 1) * 2 * P].bitcast(FP4X4),
                 lhsT_scale=v_scale[:, N + c * P : N + (c + 1) * P],
-                rhs=h_words[A4][:].bitcast(FP8X4),
-                rhs_scale=h_scale_cols(A4, slice(0, T)),
-                start=True,
+                rhs=h_words[A4][:, cols].bitcast(FP8X4),
+                rhs_scale=h_scale_cols(A4, cols),
+                start=(cols.start == 0),
                 stop=False,
             )
 
@@ -253,17 +249,19 @@ def tile_mix_save_silu_mix_gelu_kernel(
                 stop=(cols.stop == T),
             )
 
-        for c in range(PACK + 1):
-            pass_v4(c)
-        for c in range(PACK):
-            pass_v8(c, half(0))
-        pass_v4(PACK + 1)
-        for c in range(PACK):
-            pass_v8(c, half(1))
+        for h in range(2):
+            for c in range(PACK):
+                for lo in range(h * HALF, (h + 1) * HALF, P):
+                    pass_v4(c, slice(lo, lo + P))
+        for c in range(PACK, PACK + 2):
+            pass_v4(c, whole)
+        for h in range(2):
+            for c in range(PACK):
+                pass_v8(c, half(h))
         for c in range(PACK, TILES):
-            if c > PACK + 1:
-                pass_v4(c)
-            pass_v8(c, slice(0, T))
+            if c >= PACK + 2:
+                pass_v4(c, whole)
+            pass_v8(c, whole)
 
         for c in range(TILES):
             nc.scalar.activation(out=y_sb[c][:], in_=acc2[c][:], func=ACT.Gelu_apprx_tanh, bias=b_cols[:, c * SQ : c * SQ + 1])

@@ -9,6 +9,7 @@ F32 = mybir.dt.float32
 BF16 = mybir.dt.bfloat16
 I32 = mybir.dt.int32
 U32 = mybir.dt.uint32
+U16 = mybir.dt.uint16
 U8 = mybir.dt.uint8
 FP8X4 = mybir.dt.float8_e4m3fn_x4
 FP4X4 = mybir.dt.float4_e2m1fn_x4
@@ -80,31 +81,34 @@ def tile_mix_save_silu_mix_gelu_kernel(
 
         def load_scale_rows(dst, src):
             passes = src.shape[0]
-            for q in range(QUADS):
-                rows = src[:, 4 * q : 4 * q + 4, :].rearrange("k r n -> r k n")
+            rows = src.rearrange("k (q r) n -> r q k n", r=4)
+            for r in range(4):
                 nc.sync.dma_start(
-                    out=dst[32 * q : 32 * q + 4, :].bitcast(I32).rearrange("r (k n) -> r k n", k=passes),
-                    in_=rows.bitcast(I32),
+                    out=dst[r:P:SQ, :].bitcast(I32).rearrange("q (k n) -> q k n", k=passes),
+                    in_=rows[r].bitcast(I32),
                 )
 
-        load_w(A4)
-        load_scale_rows(ws_raw[:], w4_scales)
-        for k in range(2):
+        def load_x(k):
             nc.sync.dma_start(out=x_raw[k][:], in_=x[k * PASS : (k + 1) * PASS, :].rearrange("(p j) t -> p j t", j=PACK))
-        nc.scalar.dma_start(
+
+        load_w(A4)
+        load_x(0)
+        load_scale_rows(ws_raw[:], w4_scales)
+        load_x(1)
+        load_w(A8)
+        nc.sync.dma_start(out=sm_sb[:, :, 0:PACK], in_=sm.rearrange("(a p j) -> p a j", a=2, j=PACK))
+        nc.sync.dma_start(out=v8_sb[:].bitcast(I32), in_=v8_words[0].rearrange("p n i -> p (n i)").bitcast(I32))
+        nc.sync.dma_start(out=v4_sb[:].bitcast(I32), in_=v4_words[0].bitcast(I32))
+        nc.sync.dma_start(
             out=b_rows[0:P:SQ, :].rearrange("q (c i) -> q c i", i=SQ), in_=b.rearrange("(c q i) -> q c i", q=QUADS, i=SQ)
         )
-        nc.scalar.dma_start(out=sm_sb[:, :, 0:PACK], in_=sm.rearrange("(a p j) -> p a j", a=2, j=PACK))
-        load_w(A8)
-        nc.sync.dma_start(out=v4_sb[:].bitcast(I32), in_=v4_words[0].bitcast(I32))
         load_scale_rows(v_scale[:, N : 2 * N], v4_scales)
-        nc.sync.dma_start(out=v8_sb[:].bitcast(I32), in_=v8_words[0].rearrange("p n i -> p (n i)").bitcast(I32))
         load_scale_rows(v_scale[:, 0:N], v8_scales)
 
         def deal_words(a):
             nc.vector.tensor_copy(
-                out=w_words[a][:].rearrange("p (k j m e) -> p k j m e", k=2, j=PACK, e=2),
-                in_=w_raw[a][:].rearrange("p k (m j e) -> p k j m e", j=PACK, e=2),
+                out=w_words[a][:].bitcast(U16).rearrange("p (k j m) -> p k j m", k=2, j=PACK),
+                in_=w_raw[a][:].bitcast(U16).rearrange("p k (m j) -> p k j m", j=PACK),
             )
 
         def deal_scales(a):
@@ -126,19 +130,20 @@ def tile_mix_save_silu_mix_gelu_kernel(
         def quantize(words, scale, src):
             nc.vector.quantize_mx(out=words.bitcast(FP8X4), scales=scale, in_=src)
 
-        def prepare_x(k):
-            round_x(nc.scalar.copy, k, X_VEC, T)
-            round_x(nc.vector.tensor_copy, k, 0, HALF)
-            round_x(nc.vector.tensor_copy, k, HALF, X_VEC)
+        def quantize_x(k):
             for h in range(2):
                 quantize(x_words[k][:, half(h)], x_scale[k][:, half(h)], x_bf[k][:, h * HALF * PACK : (h + 1) * HALF * PACK])
 
         deal_words(A4)
+        round_x(nc.scalar.copy, 0, HALF, T)
+        round_x(nc.vector.tensor_copy, 0, 0, HALF)
         deal_scales(A4)
+        quantize_x(0)
         deal_scales(A8)
-        nc.vector.transpose(out=b_cols[:], in_=b_rows[:])
-        prepare_x(0)
-        prepare_x(1)
+        round_x(nc.scalar.copy, 1, X_VEC, T)
+        round_x(nc.vector.tensor_copy, 1, 0, HALF)
+        round_x(nc.vector.tensor_copy, 1, HALF, X_VEC)
+        quantize_x(1)
         deal_words(A8)
 
         acc1 = [[ps.tile([P, T], F32, name="acc1_%d%d" % (a, j), tag="bank%d" % (PACK * a + j)) for j in range(PACK)] for a in range(2)]
@@ -195,6 +200,7 @@ def tile_mix_save_silu_mix_gelu_kernel(
         for j in range(last):
             smooth(A4, j, whole)
             store_h(A4, j, j + 1)
+        nc.vector.transpose(out=b_cols[:], in_=b_rows[:])
         for h in range(2):
             smooth(A4, last, half(h))
         store_h(A4, last, PACK)
@@ -217,11 +223,11 @@ def tile_mix_save_silu_mix_gelu_kernel(
         for h in range(2):
             quantize_h(A8, half(h))
         store_words(A8)
-        for q in range(QUADS):
-            rows = out_3[:, 4 * q : 4 * q + 4, :].rearrange("a r t -> r a t")
+        rows = out_3.rearrange("a (q r) t -> r q a t", r=4)
+        for r in range(4):
             nc.sync.dma_start(
-                out=rows.bitcast(I32),
-                in_=h_scale[32 * q : 32 * q + 4, :].bitcast(I32).rearrange("r (a t) -> r a t", a=2),
+                out=rows[r].bitcast(I32),
+                in_=h_scale[r:P:SQ, :].bitcast(I32).rearrange("q (a t) -> q a t", a=2),
             )
 
 

@@ -26,9 +26,6 @@ TILES = N // P
 RUN = 4
 A4, A8 = 1, 0
 
-H_VEC = 368
-X_VEC = 320
-
 
 def tile_mix_save_silu_mix_gelu_kernel(
     tc, x, w4_words, w4_scales, sm, v8_words, v8_scales, v4_words, v4_scales, b, out_0, out_1, out_2, out_3
@@ -59,8 +56,9 @@ def tile_mix_save_silu_mix_gelu_kernel(
         v8_sb = tile("v8_sb", [P, 4 * N], U8)
         v4_sb = tile("v4_sb", [P, 2 * N], U8)
         v_scale = tile("v_scale", [P, 2 * N], U8)
-        s_sb = [[tile("s%d%d" % (a, j), [P, T], F32) for j in range(PACK)] for a in range(2)]
-        h_sb = [tile("h%d" % a, [P, PACK, T], F32) for a in range(2)]
+        s_sb = [tile("s%d" % g, [P, T], F32) for g in range(TILES)]
+        h4_sb = [tile("h4_%d" % h, [P, PACK, HALF], F32) for h in range(2)]
+        h8_sb = tile("h8", [P, PACK, T], F32)
         h_bf = [tile("hb%d" % a, [P, T * PACK], BF16) for a in range(2)]
         h_words = [tile("h_words%d" % a, [P, T], U32) for a in range(2)]
         h_scale = tile("h_scale", [P, 2 * T], U8)
@@ -97,18 +95,18 @@ def tile_mix_save_silu_mix_gelu_kernel(
         load_x(1)
         load_w(A8)
         nc.sync.dma_start(out=sm_sb[:, :, 0:PACK], in_=sm.rearrange("(a p j) -> p a j", a=2, j=PACK))
-        nc.sync.dma_start(out=v8_sb[:].bitcast(I32), in_=v8_words[0].rearrange("p n i -> p (n i)").bitcast(I32))
-        nc.sync.dma_start(out=v4_sb[:].bitcast(I32), in_=v4_words[0].bitcast(I32))
         nc.sync.dma_start(
             out=b_rows[0:P:SQ, :].rearrange("q (c i) -> q c i", i=SQ), in_=b.rearrange("(c q i) -> q c i", q=QUADS, i=SQ)
         )
+        nc.sync.dma_start(out=v8_sb[:].bitcast(I32), in_=v8_words[0].rearrange("p n i -> p (n i)").bitcast(I32))
+        nc.sync.dma_start(out=v4_sb[:].bitcast(I32), in_=v4_words[0].bitcast(I32))
         load_scale_rows(v_scale[:, N : 2 * N], v4_scales)
         load_scale_rows(v_scale[:, 0:N], v8_scales)
 
-        def deal_words(a):
+        def deal_words(a, lo, hi):
             nc.vector.tensor_copy(
-                out=w_words[a][:].bitcast(U16).rearrange("p (k j m) -> p k j m", k=2, j=PACK),
-                in_=w_raw[a][:].bitcast(U16).rearrange("p k (m j) -> p k j m", j=PACK),
+                out=w_words[a][:].bitcast(U16).rearrange("p (k j m) -> p k j m", k=2, j=PACK)[:, lo:hi],
+                in_=w_raw[a][:, lo:hi, :].bitcast(U16).rearrange("p k (m j) -> p k j m", j=PACK),
             )
 
         def deal_scales(a):
@@ -130,57 +128,78 @@ def tile_mix_save_silu_mix_gelu_kernel(
         def quantize(words, scale, src):
             nc.vector.quantize_mx(out=words.bitcast(FP8X4), scales=scale, in_=src)
 
-        def quantize_x(k):
-            for h in range(2):
-                quantize(x_words[k][:, half(h)], x_scale[k][:, half(h)], x_bf[k][:, h * HALF * PACK : (h + 1) * HALF * PACK])
+        def quantize_x(k, h):
+            quantize(x_words[k][:, half(h)], x_scale[k][:, half(h)], x_bf[k][:, h * HALF * PACK : (h + 1) * HALF * PACK])
 
-        deal_words(A4)
+        deal_words(A4, 0, 2)
         round_x(nc.scalar.copy, 0, HALF, T)
         round_x(nc.vector.tensor_copy, 0, 0, HALF)
         deal_scales(A4)
-        quantize_x(0)
+        for h in range(2):
+            quantize_x(0, h)
         deal_scales(A8)
-        round_x(nc.scalar.copy, 1, X_VEC, T)
-        round_x(nc.vector.tensor_copy, 1, 0, HALF)
-        round_x(nc.vector.tensor_copy, 1, HALF, X_VEC)
-        quantize_x(1)
-        deal_words(A8)
+        for h in range(2):
+            round_x(nc.scalar.copy, 1, h * HALF + P, (h + 1) * HALF)
+            round_x(nc.vector.tensor_copy, 1, h * HALF, h * HALF + P)
+        for h in range(2):
+            quantize_x(1, h)
+            deal_words(A8, h, h + 1)
 
-        acc1 = [[ps.tile([P, T], F32, name="acc1_%d%d" % (a, j), tag="bank%d" % (PACK * a + j)) for j in range(PACK)] for a in range(2)]
+        groups = [(A4, (0, 1), 0), (A4, (2, 3), 0), (A4, (0, 1), 1), (A4, (2, 3), 1)]
+        groups = groups + [(A8, (0,), None), (A8, (1,), None), (A8, (2, 3), 0), (A8, (2, 3), 1)]
+        acc1 = [ps.tile([P, T], F32, name="acc1_%d" % g, tag="bank%d" % g) for g in range(TILES)]
 
-        def pass1(a, j, k):
-            c = k * PACK + j
-            nc.tensor.matmul_mx(
-                out=acc1[a][j][:],
-                lhsT=w_words[a][:, c * 2 * P : (c + 1) * 2 * P].bitcast(FP4X4),
-                lhsT_scale=w_scale[a][:, c * P : (c + 1) * P],
-                rhs=x_words[k][:].bitcast(FP8X4),
-                rhs_scale=x_scale[k][:],
-                start=(k == 0),
-                stop=(k == 1),
-            )
+        def pass1(g, k):
+            a, rows, h = groups[g]
+            width = T if h is None else P
+            first = 0 if h is None else h * HALF
+            for i in range(T // width):
+                c = k * PACK + rows[i * width // (T // len(rows))]
+                lo = first + (i * width) % (T // len(rows))
+                nc.tensor.matmul_mx(
+                    out=acc1[g][:, i * width : (i + 1) * width],
+                    lhsT=w_words[a][:, c * 2 * P : (c + 1) * 2 * P].bitcast(FP4X4),
+                    lhsT_scale=w_scale[a][:, c * P : (c + 1) * P],
+                    rhs=x_words[k][:, lo : lo + width].bitcast(FP8X4),
+                    rhs_scale=x_scale[k][:, lo : lo + width],
+                    start=(k == 0 and i == 0),
+                    stop=(k == 1 and (i + 1) * width == T),
+                )
 
         for k in range(2):
-            for j in range(PACK):
-                pass1(A4, j, k)
-        for j in range(PACK):
+            for g in range(PACK):
+                pass1(g, k)
+        for g in range(PACK, TILES):
             for k in range(2):
-                pass1(A8, j, k)
+                pass1(g, k)
 
-        def silu(a, j, cols):
-            nc.scalar.activation(out=s_sb[a][j][:, cols], in_=acc1[a][j][:, cols], func=ACT.Silu, bias=zero[:])
+        def h_rows(a, h):
+            if a == A4:
+                return h4_sb[h][:]
+            return h8_sb[:] if h is None else h8_sb[:, :, half(h)]
 
-        def smooth(a, j, cols):
-            nc.vector.tensor_scalar(
-                out=h_sb[a][:, j, cols], in0=s_sb[a][j][:, cols], scalar1=sm_sb[:, a, j : j + 1], scalar2=None, op0=ALU.mult
-            )
+        def smooth(g):
+            a, rows, h = groups[g]
+            width = T // len(rows)
+            for i, j in enumerate(rows):
+                nc.vector.tensor_scalar(
+                    out=h_rows(a, h)[:, j, :],
+                    in0=s_sb[g][:, i * width : (i + 1) * width],
+                    scalar1=sm_sb[:, a, j : j + 1],
+                    scalar2=None,
+                    op0=ALU.mult,
+                )
 
-        def store_h(a, lo, hi):
+        def store_h(a, lo, hi, h):
             rows = out_1[a * PASS : (a + 1) * PASS, :].rearrange("(p j) t -> p j t", j=PACK)
-            nc.sync.dma_start(out=rows[:, lo:hi, :], in_=h_sb[a][:, lo:hi, :])
+            cols = whole if h is None else half(h)
+            nc.sync.dma_start(out=rows[:, lo:hi, cols], in_=h_rows(a, h)[:, lo:hi, :])
 
-        def round_h(copy, a, cols):
-            interleave(copy, h_bf[a][:, cols.start * PACK : cols.stop * PACK], h_sb[a][:, :, cols])
+        def round_h4(h):
+            interleave(nc.vector.tensor_copy, h_bf[A4][:, h * HALF * PACK : (h + 1) * HALF * PACK], h4_sb[h][:])
+
+        def round_h8(copy, lo, hi):
+            interleave(copy, h_bf[A8][:, lo * PACK : hi * PACK], h8_sb[:, :, lo:hi])
 
         def h_scale_cols(a, cols):
             return h_scale[:, a * T + cols.start : a * T + cols.stop]
@@ -192,34 +211,31 @@ def tile_mix_save_silu_mix_gelu_kernel(
             nc.sync.dma_start(out=out_2[a].rearrange("p t i -> p (t i)").bitcast(I32), in_=h_words[a][:].bitcast(I32))
 
         whole = slice(0, T)
-        last = PACK - 1
-        for a in (A4, A8):
-            for j in range(PACK):
-                silu(a, j, whole)
+        for g in range(TILES):
+            nc.scalar.activation(out=s_sb[g][:], in_=acc1[g][:], func=ACT.Silu, bias=zero[:])
 
-        for j in range(last):
-            smooth(A4, j, whole)
-            store_h(A4, j, j + 1)
+        smooth(0)
+        store_h(A4, 0, 2, 0)
+        smooth(1)
+        store_h(A4, 2, 4, 0)
         nc.vector.transpose(out=b_cols[:], in_=b_rows[:])
-        for h in range(2):
-            smooth(A4, last, half(h))
-        store_h(A4, last, PACK)
-        round_h(nc.vector.tensor_copy, A4, half(0))
-        smooth(A8, 0, whole)
-        store_h(A8, 0, 1)
+        round_h4(0)
+        smooth(2)
+        store_h(A4, 0, 2, 1)
+        smooth(3)
+        store_h(A4, 2, 4, 1)
         quantize_h(A4, half(0))
-        smooth(A8, 1, whole)
-        store_h(A8, 1, 2)
-        round_h(nc.vector.tensor_copy, A4, half(1))
-        smooth(A8, 2, whole)
-        store_h(A8, 2, last)
-        nc.scalar.activation(out=h_sb[A8][:, last, :], in_=s_sb[A8][last][:], func=ACT.Copy, scale=sm_sb[:, A8, last : last + 1])
-        store_h(A8, last, PACK)
+        smooth(4)
+        smooth(5)
+        store_h(A8, 0, 2, None)
+        smooth(6)
+        round_h8(nc.scalar.copy, 0, HALF)
+        round_h4(1)
+        smooth(7)
+        store_h(A8, 2, 4, None)
         quantize_h(A4, half(1))
         store_words(A4)
-        round_h(nc.scalar.copy, A8, slice(H_VEC, T))
-        round_h(nc.vector.tensor_copy, A8, half(0))
-        round_h(nc.vector.tensor_copy, A8, slice(HALF, H_VEC))
+        round_h8(nc.vector.tensor_copy, HALF, T)
         for h in range(2):
             quantize_h(A8, half(h))
         store_words(A8)
@@ -230,8 +246,7 @@ def tile_mix_save_silu_mix_gelu_kernel(
                 in_=h_scale[r:P:SQ, :].bitcast(I32).rearrange("q (a t) -> q a t", a=2),
             )
 
-
-        acc2 = [ps.tile([P, T], F32, name="acc2_%d" % c, tag="bank%d" % ((PACK * A4 + c) % TILES)) for c in range(TILES)]
+        acc2 = [ps.tile([P, T], F32, name="acc2_%d" % c, tag="bank%d" % c) for c in range(TILES)]
 
         def pass_v4(c, cols):
             nc.tensor.matmul_mx(
@@ -255,18 +270,20 @@ def tile_mix_save_silu_mix_gelu_kernel(
                 stop=(cols.stop == T),
             )
 
+        def half_v4(c, h):
+            for lo in range(h * HALF, (h + 1) * HALF, P):
+                pass_v4(c, slice(lo, lo + P))
+
+        for c in range(TILES):
+            half_v4(c, 0)
+        for c in range(PACK):
+            half_v4(c, 1)
         for h in range(2):
-            for c in range(PACK):
-                for lo in range(h * HALF, (h + 1) * HALF, P):
-                    pass_v4(c, slice(lo, lo + P))
-        for c in range(PACK, PACK + 2):
-            pass_v4(c, whole)
-        for h in range(2):
-            for c in range(PACK):
+            for c in range(2):
                 pass_v8(c, half(h))
-        for c in range(PACK, TILES):
-            if c >= PACK + 2:
-                pass_v4(c, whole)
+        for c in range(2, TILES):
+            if c >= PACK:
+                half_v4(c, 1)
             pass_v8(c, whole)
 
         for c in range(TILES):

@@ -24,6 +24,7 @@ QUADS = 4
 SQ = 32
 TILES = N // P
 RUN = 4
+WARM = 6
 A4, A8 = 1, 0
 
 
@@ -47,6 +48,9 @@ def tile_mix_save_silu_mix_gelu_kernel(
         x_bf = [tile("x_bf%d" % k, [P, T * PACK], BF16) for k in range(2)]
         x_words = [tile("x_words%d" % k, [P, T], U32) for k in range(2)]
         x_scale = [tile("x_scale%d" % k, [P, T], U8) for k in range(2)]
+        warm_bf = tile("warm_bf", [P, P * PACK], BF16)
+        warm_words = tile("warm_words", [P, P], U32)
+        warm_scale = tile("warm_scale", [P, T], U8)
         sm_sb = tile("sm_sb", [P, 2, 2 * PACK], F32)
         b_rows = tile("b_rows", [P, TILES * SQ], F32)
         b_cols = tile("b_cols", [P, TILES * SQ], F32)
@@ -55,7 +59,8 @@ def tile_mix_save_silu_mix_gelu_kernel(
 
         v8_sb = tile("v8_sb", [P, 4 * N], U8)
         v4_sb = tile("v4_sb", [P, 2 * N], U8)
-        v_scale = tile("v_scale", [P, 2 * N], U8)
+        v4_scale = tile("v4_scale", [P, N], U8)
+        v8_scale = tile("v8_scale", [P, N // 4], U8)
         s_sb = [tile("s%d" % g, [P, T], F32) for g in range(TILES)]
         h4_sb = [tile("h4_%d" % h, [P, PACK, HALF], F32) for h in range(2)]
         h8_sb = tile("h8", [P, PACK, T], F32)
@@ -69,8 +74,11 @@ def tile_mix_save_silu_mix_gelu_kernel(
 
         nc.vector.memset(ws_raw[:].bitcast(I32), 0)
         nc.vector.memset(zero_in[:], 0.0)
+        nc.vector.memset(warm_bf[:].bitcast(I32), 0)
+        nc.vector.memset(warm_scale[:].bitcast(I32), 0)
         nc.vector.memset(b_rows[:], 0.0)
-        nc.vector.memset(v_scale[:].bitcast(I32), 0)
+        nc.vector.memset(v4_scale[:].bitcast(I32), 0)
+        nc.vector.memset(v8_scale[:].bitcast(I32), 0)
         nc.scalar.activation(out=zero[:], in_=zero_in[:], func=ACT.Silu)
 
         def load_w(a):
@@ -86,13 +94,11 @@ def tile_mix_save_silu_mix_gelu_kernel(
                     in_=rows[r].bitcast(I32),
                 )
 
-        def load_x(k):
-            nc.sync.dma_start(out=x_raw[k][:], in_=x[k * PASS : (k + 1) * PASS, :].rearrange("(p j) t -> p j t", j=PACK))
-
+        x_rows = x.rearrange("(k p j) t -> k p j t", k=2, j=PACK)
         load_w(A4)
-        load_x(0)
+        nc.sync.dma_start(out=x_raw[0][:], in_=x_rows[0])
         load_scale_rows(ws_raw[:], w4_scales)
-        load_x(1)
+        nc.sync.dma_start(out=x_raw[1][:], in_=x_rows[1])
         load_w(A8)
         nc.sync.dma_start(out=sm_sb[:, :, 0:PACK], in_=sm.rearrange("(a p j) -> p a j", a=2, j=PACK))
         nc.sync.dma_start(
@@ -100,8 +106,7 @@ def tile_mix_save_silu_mix_gelu_kernel(
         )
         nc.sync.dma_start(out=v8_sb[:].bitcast(I32), in_=v8_words[0].rearrange("p n i -> p (n i)").bitcast(I32))
         nc.sync.dma_start(out=v4_sb[:].bitcast(I32), in_=v4_words[0].bitcast(I32))
-        load_scale_rows(v_scale[:, N : 2 * N], v4_scales)
-        load_scale_rows(v_scale[:, 0:N], v8_scales)
+        load_scale_rows(v4_scale[:], v4_scales)
 
         def deal_words(a, lo, hi):
             nc.vector.tensor_copy(
@@ -131,9 +136,22 @@ def tile_mix_save_silu_mix_gelu_kernel(
         def quantize_x(k, h):
             quantize(x_words[k][:, half(h)], x_scale[k][:, half(h)], x_bf[k][:, h * HALF * PACK : (h + 1) * HALF * PACK])
 
+        quantize(warm_words[:], warm_scale[:, 0:P], warm_bf[:])
+        warm_acc = ps.tile([P, T], F32, name="warm_acc", tag="bank7")
+        for i in range(WARM):
+            nc.tensor.matmul_mx(
+                out=warm_acc[:],
+                lhsT=warm_words[:].bitcast(FP8X4),
+                lhsT_scale=warm_scale[:, 0:P],
+                rhs=w_raw[A4][:, 0, :].bitcast(FP4X4),
+                rhs_scale=warm_scale[:],
+                start=True,
+                stop=True,
+            )
         deal_words(A4, 0, 2)
-        round_x(nc.scalar.copy, 0, HALF, T)
-        round_x(nc.vector.tensor_copy, 0, 0, HALF)
+        for h in range(2):
+            round_x(nc.scalar.copy, 0, h * HALF + P, (h + 1) * HALF)
+            round_x(nc.vector.tensor_copy, 0, h * HALF, h * HALF + P)
         deal_scales(A4)
         for h in range(2):
             quantize_x(0, h)
@@ -168,9 +186,6 @@ def tile_mix_save_silu_mix_gelu_kernel(
 
         for k in range(2):
             for g in range(PACK):
-                pass1(g, k)
-        for g in range(PACK, TILES):
-            for k in range(2):
                 pass1(g, k)
 
         def h_rows(a, h):
@@ -211,11 +226,21 @@ def tile_mix_save_silu_mix_gelu_kernel(
             nc.sync.dma_start(out=out_2[a].rearrange("p t i -> p (t i)").bitcast(I32), in_=h_words[a][:].bitcast(I32))
 
         whole = slice(0, T)
-        for g in range(TILES):
+
+        def silu(g):
             nc.scalar.activation(out=s_sb[g][:], in_=acc1[g][:], func=ACT.Silu, bias=zero[:])
 
+        silu(0)
         smooth(0)
         store_h(A4, 0, 2, 0)
+        for k in range(2):
+            for g in (4, 5):
+                pass1(g, k)
+        for g in (6, 7):
+            for k in range(2):
+                pass1(g, k)
+        for g in range(1, TILES):
+            silu(g)
         smooth(1)
         store_h(A4, 2, 4, 0)
         nc.vector.transpose(out=b_cols[:], in_=b_rows[:])
@@ -224,6 +249,11 @@ def tile_mix_save_silu_mix_gelu_kernel(
         store_h(A4, 0, 2, 1)
         smooth(3)
         store_h(A4, 2, 4, 1)
+        for q in range(QUADS):
+            nc.sync.dma_start(
+                out=v8_scale[SQ * q : SQ * q + 16, :].bitcast(I32),
+                in_=v8_scales[0, 4 * q : 4 * q + 4, :].bitcast(I32).rearrange("r (g n) -> g r n", g=4),
+            )
         quantize_h(A4, half(0))
         smooth(4)
         smooth(5)
@@ -252,7 +282,7 @@ def tile_mix_save_silu_mix_gelu_kernel(
             nc.tensor.matmul_mx(
                 out=acc2[c][:, cols],
                 lhsT=v4_sb[:, c * 2 * P : (c + 1) * 2 * P].bitcast(FP4X4),
-                lhsT_scale=v_scale[:, N + c * P : N + (c + 1) * P],
+                lhsT_scale=v4_scale[:, c * P : (c + 1) * P],
                 rhs=h_words[A4][:, cols].bitcast(FP8X4),
                 rhs_scale=h_scale_cols(A4, cols),
                 start=(cols.start == 0),
@@ -263,7 +293,7 @@ def tile_mix_save_silu_mix_gelu_kernel(
             nc.tensor.matmul_mx(
                 out=acc2[c][:, cols],
                 lhsT=v8_sb[:, c * 4 * P : (c + 1) * 4 * P].bitcast(FP8X4),
-                lhsT_scale=v_scale[:, c * P : (c + 1) * P],
+                lhsT_scale=v8_scale[4 * (c // 2) : P, (c % 2) * P : (c % 2 + 1) * P],
                 rhs=h_words[A8][:, cols].bitcast(FP8X4),
                 rhs_scale=h_scale_cols(A8, cols),
                 start=False,

@@ -24,7 +24,6 @@ QUADS = 4
 SQ = 32
 TILES = N // P
 RUN = 4
-WARM = 6
 A4, A8 = 1, 0
 
 
@@ -48,9 +47,6 @@ def tile_mix_save_silu_mix_gelu_kernel(
         x_bf = [tile("x_bf%d" % k, [P, T * PACK], BF16) for k in range(2)]
         x_words = [tile("x_words%d" % k, [P, T], U32) for k in range(2)]
         x_scale = [tile("x_scale%d" % k, [P, T], U8) for k in range(2)]
-        warm_bf = tile("warm_bf", [P, P * PACK], BF16)
-        warm_words = tile("warm_words", [P, P], U32)
-        warm_scale = tile("warm_scale", [P, T], U8)
         sm_sb = tile("sm_sb", [P, 2, 2 * PACK], F32)
         b_rows = tile("b_rows", [P, TILES * SQ], F32)
         b_cols = tile("b_cols", [P, TILES * SQ], F32)
@@ -74,8 +70,6 @@ def tile_mix_save_silu_mix_gelu_kernel(
 
         nc.vector.memset(ws_raw[:].bitcast(I32), 0)
         nc.vector.memset(zero_in[:], 0.0)
-        nc.vector.memset(warm_bf[:].bitcast(I32), 0)
-        nc.vector.memset(warm_scale[:].bitcast(I32), 0)
         nc.vector.memset(b_rows[:], 0.0)
         nc.vector.memset(v4_scale[:].bitcast(I32), 0)
         nc.vector.memset(v8_scale[:].bitcast(I32), 0)
@@ -136,18 +130,6 @@ def tile_mix_save_silu_mix_gelu_kernel(
         def quantize_x(k, h):
             quantize(x_words[k][:, half(h)], x_scale[k][:, half(h)], x_bf[k][:, h * HALF * PACK : (h + 1) * HALF * PACK])
 
-        quantize(warm_words[:], warm_scale[:, 0:P], warm_bf[:])
-        warm_acc = ps.tile([P, T], F32, name="warm_acc", tag="bank7")
-        for i in range(WARM):
-            nc.tensor.matmul_mx(
-                out=warm_acc[:],
-                lhsT=warm_words[:].bitcast(FP8X4),
-                lhsT_scale=warm_scale[:, 0:P],
-                rhs=w_raw[A4][:, 0, :].bitcast(FP4X4),
-                rhs_scale=warm_scale[:],
-                start=True,
-                stop=True,
-            )
         deal_words(A4, 0, 2)
         for h in range(2):
             round_x(nc.scalar.copy, 0, h * HALF + P, (h + 1) * HALF)

@@ -24,6 +24,7 @@ QUADS = 4
 SQ = 32
 TILES = N // P
 RUN = 4
+SHARE = 224
 A4, A8 = 1, 0
 
 
@@ -48,11 +49,10 @@ def tile_mix_save_silu_mix_gelu_kernel(
         x_words = [tile("x_words%d" % k, [P, T], U32) for k in range(2)]
         x_scale = [tile("x_scale%d" % k, [P, T], U8) for k in range(2)]
         sm_sb = tile("sm_sb", [P, 2, 2 * PACK], F32)
-        b_rows = tile("b_rows", [P, TILES * SQ], F32)
-        b_cols = tile("b_cols", [P, TILES * SQ], F32)
+        b_rows = tile("b_rows", [P, SQ], F32)
+        b_cols = tile("b_cols", [P, SQ], F32)
         zero_in = tile("zero_in", [P, 1], F32)
         zero = tile("zero", [P, 1], F32)
-
         v8_sb = tile("v8_sb", [P, 4 * N], U8)
         v4_sb = tile("v4_sb", [P, 2 * N], U8)
         v4_scale = tile("v4_scale", [P, N], U8)
@@ -60,13 +60,15 @@ def tile_mix_save_silu_mix_gelu_kernel(
         s_sb = [tile("s%d" % g, [P, T], F32) for g in range(TILES)]
         h4_sb = [tile("h4_%d" % h, [P, PACK, HALF], F32) for h in range(2)]
         h8_sb = tile("h8", [P, PACK, T], F32)
-        h_bf = [tile("hb%d" % a, [P, T * PACK], BF16) for a in range(2)]
+        h_bf = [[tile("hb%d_%d" % (a, h), [P, HALF * PACK], BF16) for h in range(2)] for a in range(2)]
         h_words = [tile("h_words%d" % a, [P, T], U32) for a in range(2)]
         h_scale = tile("h_scale", [P, 2 * T], U8)
         y_sb = [tile("y%d" % c, [P, T], F32) for c in range(TILES)]
 
         def half(h):
             return slice(h * HALF, (h + 1) * HALF)
+
+        whole = slice(0, T)
 
         nc.vector.memset(ws_raw[:].bitcast(I32), 0)
         nc.vector.memset(zero_in[:], 0.0)
@@ -95,12 +97,15 @@ def tile_mix_save_silu_mix_gelu_kernel(
         nc.sync.dma_start(out=x_raw[1][:], in_=x_rows[1])
         load_w(A8)
         nc.sync.dma_start(out=sm_sb[:, :, 0:PACK], in_=sm.rearrange("(a p j) -> p a j", a=2, j=PACK))
-        nc.sync.dma_start(
-            out=b_rows[0:P:SQ, :].rearrange("q (c i) -> q c i", i=SQ), in_=b.rearrange("(c q i) -> q c i", q=QUADS, i=SQ)
-        )
+        nc.sync.dma_start(out=b_rows[0:P:PACK, :], in_=b.rearrange("(c q i) -> q c i", q=QUADS, i=SQ))
         nc.sync.dma_start(out=v8_sb[:].bitcast(I32), in_=v8_words[0].rearrange("p n i -> p (n i)").bitcast(I32))
-        nc.sync.dma_start(out=v4_sb[:].bitcast(I32), in_=v4_words[0].bitcast(I32))
         load_scale_rows(v4_scale[:], v4_scales)
+        nc.sync.dma_start(out=v4_sb[:].bitcast(I32), in_=v4_words[0].bitcast(I32))
+        for q in range(QUADS):
+            nc.sync.dma_start(
+                out=v8_scale[SQ * q : SQ * q + 16, :].bitcast(I32),
+                in_=v8_scales[0, 4 * q : 4 * q + 4, :].bitcast(I32).rearrange("r (g n) -> g r n", g=4),
+            )
 
         def deal_words(a, lo, hi):
             nc.vector.tensor_copy(
@@ -130,17 +135,18 @@ def tile_mix_save_silu_mix_gelu_kernel(
         def quantize_x(k, h):
             quantize(x_words[k][:, half(h)], x_scale[k][:, half(h)], x_bf[k][:, h * HALF * PACK : (h + 1) * HALF * PACK])
 
+        vec = nc.vector.tensor_copy
         deal_words(A4, 0, 2)
         for h in range(2):
             round_x(nc.scalar.copy, 0, h * HALF + P, (h + 1) * HALF)
-            round_x(nc.vector.tensor_copy, 0, h * HALF, h * HALF + P)
+            round_x(vec, 0, h * HALF, h * HALF + P)
         deal_scales(A4)
         for h in range(2):
             quantize_x(0, h)
         deal_scales(A8)
         for h in range(2):
             round_x(nc.scalar.copy, 1, h * HALF + P, (h + 1) * HALF)
-            round_x(nc.vector.tensor_copy, 1, h * HALF, h * HALF + P)
+            round_x(vec, 1, h * HALF, h * HALF + P)
         for h in range(2):
             quantize_x(1, h)
             deal_words(A8, h, h + 1)
@@ -151,29 +157,27 @@ def tile_mix_save_silu_mix_gelu_kernel(
 
         def pass1(g, k):
             a, rows, h = groups[g]
-            width = T if h is None else P
-            first = 0 if h is None else h * HALF
-            for i in range(T // width):
-                c = k * PACK + rows[i * width // (T // len(rows))]
-                lo = first + (i * width) % (T // len(rows))
+            cols = whole if h is None else half(h)
+            width = T // len(rows)
+            for i, j in enumerate(rows):
+                c = k * PACK + j
                 nc.tensor.matmul_mx(
                     out=acc1[g][:, i * width : (i + 1) * width],
                     lhsT=w_words[a][:, c * 2 * P : (c + 1) * 2 * P].bitcast(FP4X4),
                     lhsT_scale=w_scale[a][:, c * P : (c + 1) * P],
-                    rhs=x_words[k][:, lo : lo + width].bitcast(FP8X4),
-                    rhs_scale=x_scale[k][:, lo : lo + width],
+                    rhs=x_words[k][:, cols].bitcast(FP8X4),
+                    rhs_scale=x_scale[k][:, cols],
                     start=(k == 0 and i == 0),
-                    stop=(k == 1 and (i + 1) * width == T),
+                    stop=(k == 1 and i == len(rows) - 1),
                 )
-
-        for k in range(2):
-            for g in range(PACK):
-                pass1(g, k)
 
         def h_rows(a, h):
             if a == A4:
                 return h4_sb[h][:]
             return h8_sb[:] if h is None else h8_sb[:, :, half(h)]
+
+        def silu(g):
+            nc.scalar.activation(out=s_sb[g][:], in_=acc1[g][:], func=ACT.Silu, bias=zero[:])
 
         def smooth(g):
             a, rows, h = groups[g]
@@ -192,64 +196,54 @@ def tile_mix_save_silu_mix_gelu_kernel(
             cols = whole if h is None else half(h)
             nc.sync.dma_start(out=rows[:, lo:hi, cols], in_=h_rows(a, h)[:, lo:hi, :])
 
-        def round_h4(h):
-            interleave(nc.vector.tensor_copy, h_bf[A4][:, h * HALF * PACK : (h + 1) * HALF * PACK], h4_sb[h][:])
-
-        def round_h8(copy, lo, hi):
-            interleave(copy, h_bf[A8][:, lo * PACK : hi * PACK], h8_sb[:, :, lo:hi])
+        def round_h(copy, a, h, lo, hi):
+            interleave(copy, h_bf[a][h][:, lo * PACK : hi * PACK], h_rows(a, h)[:, :, lo:hi])
 
         def h_scale_cols(a, cols):
             return h_scale[:, a * T + cols.start : a * T + cols.stop]
 
-        def quantize_h(a, cols):
-            quantize(h_words[a][:, cols], h_scale_cols(a, cols), h_bf[a][:, cols.start * PACK : cols.stop * PACK])
+        def quantize_h(a, h):
+            quantize(h_words[a][:, half(h)], h_scale_cols(a, half(h)), h_bf[a][h][:])
 
         def store_words(a):
             nc.sync.dma_start(out=out_2[a].rearrange("p t i -> p (t i)").bitcast(I32), in_=h_words[a][:].bitcast(I32))
 
-        whole = slice(0, T)
-
-        def silu(g):
-            nc.scalar.activation(out=s_sb[g][:], in_=acc1[g][:], func=ACT.Silu, bias=zero[:])
-
+        for k in range(2):
+            for g in range(PACK):
+                pass1(g, k)
         silu(0)
         smooth(0)
         store_h(A4, 0, 2, 0)
-        for k in range(2):
-            for g in (4, 5):
-                pass1(g, k)
-        for g in (6, 7):
+        nc.vector.transpose(out=b_cols[:], in_=b_rows[:])
+        for g in range(PACK, TILES):
             for k in range(2):
                 pass1(g, k)
         for g in range(1, TILES):
             silu(g)
         smooth(1)
         store_h(A4, 2, 4, 0)
-        nc.vector.transpose(out=b_cols[:], in_=b_rows[:])
-        round_h4(0)
+        round_h(vec, A4, 0, 0, P)
         smooth(2)
         store_h(A4, 0, 2, 1)
+        round_h(vec, A4, 0, P, HALF)
         smooth(3)
         store_h(A4, 2, 4, 1)
-        for q in range(QUADS):
-            nc.sync.dma_start(
-                out=v8_scale[SQ * q : SQ * q + 16, :].bitcast(I32),
-                in_=v8_scales[0, 4 * q : 4 * q + 4, :].bitcast(I32).rearrange("r (g n) -> g r n", g=4),
-            )
-        quantize_h(A4, half(0))
+        quantize_h(A4, 0)
         smooth(4)
+        round_h(vec, A4, 1, 0, P)
         smooth(5)
         store_h(A8, 0, 2, None)
         smooth(6)
-        round_h8(nc.scalar.copy, 0, HALF)
-        round_h4(1)
+        round_h(nc.scalar.copy, A8, 0, 0, SHARE)
+        round_h(vec, A4, 1, P, HALF)
         smooth(7)
         store_h(A8, 2, 4, None)
-        quantize_h(A4, half(1))
+        quantize_h(A4, 1)
         store_words(A4)
-        round_h8(nc.vector.tensor_copy, HALF, T)
-        for h in range(2):
-            quantize_h(A8, half(h))
+        round_h(vec, A8, 0, SHARE, HALF)
+        round_h(vec, A8, 1, 0, HALF)
+        quantize_h(A8, 0)
+        quantize_h(A8, 1)
         store_words(A8)
         rows = out_3.rearrange("a (q r) t -> r q a t", r=4)
         for r in range(4):
@@ -282,22 +276,18 @@ def tile_mix_save_silu_mix_gelu_kernel(
                 stop=(cols.stop == T),
             )
 
-        def half_v4(c, h):
-            for lo in range(h * HALF, (h + 1) * HALF, P):
-                pass_v4(c, slice(lo, lo + P))
-
         for c in range(TILES):
-            half_v4(c, 0)
-        for c in range(PACK):
-            half_v4(c, 1)
-        for h in range(2):
-            for c in range(2):
-                pass_v8(c, half(h))
+            pass_v4(c, half(0))
+        for c in range(2):
+            pass_v4(c, half(1))
+        for c in range(2):
+            pass_v8(c, half(0))
+        for c in range(2):
+            pass_v8(c, half(1))
         for c in range(2, TILES):
-            if c >= PACK:
-                half_v4(c, 1)
+            pass_v4(c, half(1))
             pass_v8(c, whole)
 
         for c in range(TILES):
-            nc.scalar.activation(out=y_sb[c][:], in_=acc2[c][:], func=ACT.Gelu_apprx_tanh, bias=b_cols[:, c * SQ : c * SQ + 1])
+            nc.scalar.activation(out=y_sb[c][:], in_=acc2[c][:], func=ACT.Gelu_apprx_tanh, bias=b_cols[:, c * PACK : c * PACK + 1])
             nc.sync.dma_start(out=out_0[c * P : (c + 1) * P, :], in_=y_sb[c][:])

@@ -24,7 +24,10 @@ QUADS = 4
 SQ = 32
 TILES = N // P
 RUN = 4
-SHARE = 224
+SHARE = 192
+EARLY = 6
+X_SPLIT = 160
+WARM = 3
 A4, A8 = 1, 0
 
 
@@ -44,7 +47,8 @@ def tile_mix_save_silu_mix_gelu_kernel(
         w_words = [tile("w_words%d" % a, [P, 2 * PACK * 2 * P], U8) for a in range(2)]
         ws_raw = tile("ws_raw", [P, 2 * R], U8)
         w_scale = [tile("w_scale%d" % a, [P, 2 * PACK * P], U8) for a in range(2)]
-        x_raw = [tile("x_raw%d" % k, [P, PACK, T], F32) for k in range(2)]
+        x0_raw = tile("x0_raw", [P, PACK, T], F32)
+        x1_raw = [tile("x1_raw%d" % h, [P, PACK, HALF], F32) for h in range(2)]
         x_bf = [tile("x_bf%d" % k, [P, T * PACK], BF16) for k in range(2)]
         x_words = [tile("x_words%d" % k, [P, T], U32) for k in range(2)]
         x_scale = [tile("x_scale%d" % k, [P, T], U8) for k in range(2)]
@@ -53,6 +57,9 @@ def tile_mix_save_silu_mix_gelu_kernel(
         b_cols = tile("b_cols", [P, SQ], F32)
         zero_in = tile("zero_in", [P, 1], F32)
         zero = tile("zero", [P, 1], F32)
+        warm_bf = tile("warm_bf", [P, T * PACK], BF16)
+        warm_words = tile("warm_words", [P, T], U32)
+        warm_scale = tile("warm_scale", [P, T], U8)
         v8_sb = tile("v8_sb", [P, 4 * N], U8)
         v4_sb = tile("v4_sb", [P, 2 * N], U8)
         v4_scale = tile("v4_scale", [P, N], U8)
@@ -75,6 +82,7 @@ def tile_mix_save_silu_mix_gelu_kernel(
         nc.vector.memset(b_rows[:], 0.0)
         nc.vector.memset(v4_scale[:].bitcast(I32), 0)
         nc.vector.memset(v8_scale[:].bitcast(I32), 0)
+        nc.vector.memset(warm_bf[:].bitcast(I32), 0)
         nc.scalar.activation(out=zero[:], in_=zero_in[:], func=ACT.Silu)
 
         def load_w(a):
@@ -92,20 +100,17 @@ def tile_mix_save_silu_mix_gelu_kernel(
 
         x_rows = x.rearrange("(k p j) t -> k p j t", k=2, j=PACK)
         load_w(A4)
-        nc.sync.dma_start(out=x_raw[0][:], in_=x_rows[0])
+        nc.sync.dma_start(out=x0_raw[:, 0:2, :], in_=x_rows[0][:, 0:2, :])
         load_scale_rows(ws_raw[:], w4_scales)
-        nc.sync.dma_start(out=x_raw[1][:], in_=x_rows[1])
+        nc.sync.dma_start(out=x0_raw[:, 2:4, :], in_=x_rows[0][:, 2:4, :])
+        for h in range(2):
+            nc.sync.dma_start(out=x1_raw[h][:], in_=x_rows[1][:, :, half(h)])
         load_w(A8)
         nc.sync.dma_start(out=sm_sb[:, :, 0:PACK], in_=sm.rearrange("(a p j) -> p a j", a=2, j=PACK))
         nc.sync.dma_start(out=b_rows[0:P:PACK, :], in_=b.rearrange("(c q i) -> q c i", q=QUADS, i=SQ))
         nc.sync.dma_start(out=v8_sb[:].bitcast(I32), in_=v8_words[0].rearrange("p n i -> p (n i)").bitcast(I32))
-        load_scale_rows(v4_scale[:], v4_scales)
         nc.sync.dma_start(out=v4_sb[:].bitcast(I32), in_=v4_words[0].bitcast(I32))
-        for q in range(QUADS):
-            nc.sync.dma_start(
-                out=v8_scale[SQ * q : SQ * q + 16, :].bitcast(I32),
-                in_=v8_scales[0, 4 * q : 4 * q + 4, :].bitcast(I32).rearrange("r (g n) -> g r n", g=4),
-            )
+        load_scale_rows(v4_scale[:], v4_scales)
 
         def deal_words(a, lo, hi):
             nc.vector.tensor_copy(
@@ -126,8 +131,11 @@ def tile_mix_save_silu_mix_gelu_kernel(
                 in_=src.rearrange("p j (c i) -> p c j i", i=RUN),
             )
 
-        def round_x(copy, k, lo, hi):
-            interleave(copy, x_bf[k][:, lo * PACK : hi * PACK], x_raw[k][:, :, lo:hi])
+        def round_x0(copy, lo, hi):
+            interleave(copy, x_bf[0][:, lo * PACK : hi * PACK], x0_raw[:, :, lo:hi])
+
+        def round_x1(copy, h, lo, hi):
+            interleave(copy, x_bf[1][:, (h * HALF + lo) * PACK : (h * HALF + hi) * PACK], x1_raw[h][:, :, lo:hi])
 
         def quantize(words, scale, src):
             nc.vector.quantize_mx(out=words.bitcast(FP8X4), scales=scale, in_=src)
@@ -137,19 +145,32 @@ def tile_mix_save_silu_mix_gelu_kernel(
 
         vec = nc.vector.tensor_copy
         deal_words(A4, 0, 2)
-        for h in range(2):
-            round_x(nc.scalar.copy, 0, h * HALF + P, (h + 1) * HALF)
-            round_x(vec, 0, h * HALF, h * HALF + P)
+        quantize(warm_words[:], warm_scale[:], warm_bf[:])
+        warm_acc = ps.tile([P, T], F32, name="warm_acc", tag="bank%d" % (TILES - 1))
+        for i in range(WARM):
+            nc.tensor.matmul_mx(
+                out=warm_acc[:],
+                lhsT=warm_words[:, 0:P].bitcast(FP8X4),
+                lhsT_scale=warm_scale[:, 0:P],
+                rhs=warm_words[:].bitcast(FP8X4),
+                rhs_scale=warm_scale[:],
+                start=True,
+                stop=True,
+            )
         deal_scales(A4)
-        for h in range(2):
-            quantize_x(0, h)
         deal_scales(A8)
         for h in range(2):
-            round_x(nc.scalar.copy, 1, h * HALF + P, (h + 1) * HALF)
-            round_x(vec, 1, h * HALF, h * HALF + P)
+            round_x0(nc.scalar.copy, h * HALF + P, (h + 1) * HALF)
+            round_x0(vec, h * HALF, h * HALF + P)
+        quantize_x(0, 0)
         for h in range(2):
-            quantize_x(1, h)
-            deal_words(A8, h, h + 1)
+            round_x1(nc.scalar.copy, h, X_SPLIT, HALF)
+        round_x1(vec, 0, 0, X_SPLIT)
+        quantize_x(0, 1)
+        quantize_x(1, 0)
+        round_x1(vec, 1, 0, X_SPLIT)
+        quantize_x(1, 1)
+        deal_words(A8, 0, 1)
 
         groups = [(A4, (0, 1), 0), (A4, (2, 3), 0), (A4, (0, 1), 1), (A4, (2, 3), 1)]
         groups = groups + [(A8, (0,), None), (A8, (1,), None), (A8, (2, 3), 0), (A8, (2, 3), 1)]
@@ -208,13 +229,12 @@ def tile_mix_save_silu_mix_gelu_kernel(
         def store_words(a):
             nc.sync.dma_start(out=out_2[a].rearrange("p t i -> p (t i)").bitcast(I32), in_=h_words[a][:].bitcast(I32))
 
-        for k in range(2):
-            for g in range(PACK):
-                pass1(g, k)
+        for g, k in ((0, 0), (1, 0), (2, 0), (0, 1), (1, 1), (3, 0), (2, 1), (3, 1)):
+            pass1(g, k)
         silu(0)
         smooth(0)
         store_h(A4, 0, 2, 0)
-        nc.vector.transpose(out=b_cols[:], in_=b_rows[:])
+        deal_words(A8, 1, 2)
         for g in range(PACK, TILES):
             for k in range(2):
                 pass1(g, k)
@@ -222,6 +242,11 @@ def tile_mix_save_silu_mix_gelu_kernel(
             silu(g)
         smooth(1)
         store_h(A4, 2, 4, 0)
+        for q in range(QUADS):
+            nc.sync.dma_start(
+                out=v8_scale[SQ * q : SQ * q + 16, :].bitcast(I32),
+                in_=v8_scales[0, 4 * q : 4 * q + 4, :].bitcast(I32).rearrange("r (g n) -> g r n", g=4),
+            )
         round_h(vec, A4, 0, 0, P)
         smooth(2)
         store_h(A4, 0, 2, 1)
@@ -229,6 +254,7 @@ def tile_mix_save_silu_mix_gelu_kernel(
         smooth(3)
         store_h(A4, 2, 4, 1)
         quantize_h(A4, 0)
+        nc.vector.transpose(out=b_cols[:], in_=b_rows[:])
         smooth(4)
         round_h(vec, A4, 1, 0, P)
         smooth(5)
@@ -278,14 +304,15 @@ def tile_mix_save_silu_mix_gelu_kernel(
 
         for c in range(TILES):
             pass_v4(c, half(0))
-        for c in range(2):
+        for c in range(EARLY):
             pass_v4(c, half(1))
         for c in range(2):
             pass_v8(c, half(0))
         for c in range(2):
             pass_v8(c, half(1))
         for c in range(2, TILES):
-            pass_v4(c, half(1))
+            if c >= EARLY:
+                pass_v4(c, half(1))
             pass_v8(c, whole)
 
         for c in range(TILES):

@@ -24,7 +24,7 @@ QUADS = 4
 SQ = 32
 TILES = N // P
 RUN = 4
-SHARE = 192
+SHARE = 160
 EARLY = 6
 X_SPLIT = 160
 WARM = 3
@@ -65,8 +65,7 @@ def tile_mix_save_silu_mix_gelu_kernel(
         v4_scale = tile("v4_scale", [P, N], U8)
         v8_scale = tile("v8_scale", [P, N // 4], U8)
         s_sb = [tile("s%d" % g, [P, T], F32) for g in range(TILES)]
-        h4_sb = [tile("h4_%d" % h, [P, PACK, HALF], F32) for h in range(2)]
-        h8_sb = tile("h8", [P, PACK, T], F32)
+        h_sb = [tile("h%d" % a, [P, PACK, T], F32) for a in range(2)]
         h_bf = [[tile("hb%d_%d" % (a, h), [P, HALF * PACK], BF16) for h in range(2)] for a in range(2)]
         h_words = [tile("h_words%d" % a, [P, T], U32) for a in range(2)]
         h_scale = tile("h_scale", [P, 2 * T], U8)
@@ -193,9 +192,7 @@ def tile_mix_save_silu_mix_gelu_kernel(
                 )
 
         def h_rows(a, h):
-            if a == A4:
-                return h4_sb[h][:]
-            return h8_sb[:] if h is None else h8_sb[:, :, half(h)]
+            return h_sb[a][:] if h is None else h_sb[a][:, :, half(h)]
 
         def silu(g):
             nc.scalar.activation(out=s_sb[g][:], in_=acc1[g][:], func=ACT.Silu, bias=zero[:])
@@ -241,7 +238,6 @@ def tile_mix_save_silu_mix_gelu_kernel(
         for g in range(1, TILES):
             silu(g)
         smooth(1)
-        store_h(A4, 2, 4, 0)
         for q in range(QUADS):
             nc.sync.dma_start(
                 out=v8_scale[SQ * q : SQ * q + 16, :].bitcast(I32),
@@ -252,13 +248,13 @@ def tile_mix_save_silu_mix_gelu_kernel(
         store_h(A4, 0, 2, 1)
         round_h(vec, A4, 0, P, HALF)
         smooth(3)
-        store_h(A4, 2, 4, 1)
+        store_h(A4, 2, 4, None)
         quantize_h(A4, 0)
-        nc.vector.transpose(out=b_cols[:], in_=b_rows[:])
         smooth(4)
-        round_h(vec, A4, 1, 0, P)
+        nc.vector.transpose(out=b_cols[:], in_=b_rows[:])
         smooth(5)
         store_h(A8, 0, 2, None)
+        round_h(vec, A4, 1, 0, P)
         smooth(6)
         round_h(nc.scalar.copy, A8, 0, 0, SHARE)
         round_h(vec, A4, 1, P, HALF)
@@ -278,43 +274,59 @@ def tile_mix_save_silu_mix_gelu_kernel(
                 in_=h_scale[r:P:SQ, :].bitcast(I32).rearrange("q (a t) -> q a t", a=2),
             )
 
-        acc2 = [ps.tile([P, T], F32, name="acc2_%d" % c, tag="bank%d" % c) for c in range(TILES)]
+        first = [ps.tile([P, T], F32, name="first%d" % h, tag="bank%d" % h) for h in range(2)]
+        acc2 = {c: ps.tile([P, T], F32, name="acc2_%d" % c, tag="bank%d" % (c + 1)) for c in range(1, TILES - 1)}
+
+        def bank(c, cols):
+            return first[cols.start // HALF] if c == 0 else acc2[c]
 
         def pass_v4(c, cols):
             nc.tensor.matmul_mx(
-                out=acc2[c][:, cols],
+                out=bank(c, cols)[:, cols],
                 lhsT=v4_sb[:, c * 2 * P : (c + 1) * 2 * P].bitcast(FP4X4),
                 lhsT_scale=v4_scale[:, c * P : (c + 1) * P],
                 rhs=h_words[A4][:, cols].bitcast(FP8X4),
                 rhs_scale=h_scale_cols(A4, cols),
-                start=(cols.start == 0),
+                start=(c == 0 or cols.start == 0),
                 stop=False,
             )
 
         def pass_v8(c, cols):
             nc.tensor.matmul_mx(
-                out=acc2[c][:, cols],
+                out=bank(c, cols)[:, cols],
                 lhsT=v8_sb[:, c * 4 * P : (c + 1) * 4 * P].bitcast(FP8X4),
                 lhsT_scale=v8_scale[4 * (c // 2) : P, (c % 2) * P : (c % 2 + 1) * P],
                 rhs=h_words[A8][:, cols].bitcast(FP8X4),
                 rhs_scale=h_scale_cols(A8, cols),
                 start=False,
-                stop=(cols.stop == T),
+                stop=(c == 0 or cols.stop == T),
             )
 
-        for c in range(TILES):
+        def gelu(c, cols):
+            nc.scalar.activation(
+                out=y_sb[c][:, cols], in_=bank(c, cols)[:, cols], func=ACT.Gelu_apprx_tanh, bias=b_cols[:, c * PACK : c * PACK + 1]
+            )
+
+        def store_y(c):
+            nc.sync.dma_start(out=out_0[c * P : (c + 1) * P, :], in_=y_sb[c][:])
+
+        for c in range(TILES - 1):
             pass_v4(c, half(0))
         for c in range(EARLY):
             pass_v4(c, half(1))
-        for c in range(2):
-            pass_v8(c, half(0))
-        for c in range(2):
-            pass_v8(c, half(1))
+        for h in range(2):
+            for c in range(2):
+                pass_v8(c, half(h))
+        for h in range(2):
+            gelu(0, half(h))
+        store_y(0)
+        acc2[TILES - 1] = ps.tile([P, T], F32, name="acc2_last", tag="bank0")
         for c in range(2, TILES):
-            if c >= EARLY:
+            if c == TILES - 1:
+                pass_v4(c, whole)
+            elif c >= EARLY:
                 pass_v4(c, half(1))
             pass_v8(c, whole)
-
-        for c in range(TILES):
-            nc.scalar.activation(out=y_sb[c][:], in_=acc2[c][:], func=ACT.Gelu_apprx_tanh, bias=b_cols[:, c * PACK : c * PACK + 1])
-            nc.sync.dma_start(out=out_0[c * P : (c + 1) * P, :], in_=y_sb[c][:])
+        for c in range(1, TILES):
+            gelu(c, whole)
+            store_y(c)

@@ -106,9 +106,14 @@ def tile_mix_save_silu_mix_gelu_kernel(
             nc.sync.dma_start(out=x1_raw[h][:], in_=x_rows[1][:, :, half(h)])
         load_w(A8)
         nc.sync.dma_start(out=sm_sb[:, :, 0:PACK], in_=sm.rearrange("(a p j) -> p a j", a=2, j=PACK))
-        nc.sync.dma_start(out=b_rows[0:P:PACK, :], in_=b.rearrange("(c q i) -> q c i", q=QUADS, i=SQ))
+        for q in range(QUADS):
+            nc.sync.dma_start(
+                out=v8_scale[SQ * q : SQ * q + 16, :].bitcast(I32),
+                in_=v8_scales[0, 4 * q : 4 * q + 4, :].bitcast(I32).rearrange("r (g n) -> g r n", g=4),
+            )
         nc.sync.dma_start(out=v8_sb[:].bitcast(I32), in_=v8_words[0].rearrange("p n i -> p (n i)").bitcast(I32))
         nc.sync.dma_start(out=v4_sb[:].bitcast(I32), in_=v4_words[0].bitcast(I32))
+        nc.sync.dma_start(out=b_rows[0:P:PACK, :], in_=b.rearrange("(c q i) -> q c i", q=QUADS, i=SQ))
         load_scale_rows(v4_scale[:], v4_scales)
 
         def deal_words(a, lo, hi):
@@ -238,17 +243,13 @@ def tile_mix_save_silu_mix_gelu_kernel(
         for g in range(1, TILES):
             silu(g)
         smooth(1)
-        for q in range(QUADS):
-            nc.sync.dma_start(
-                out=v8_scale[SQ * q : SQ * q + 16, :].bitcast(I32),
-                in_=v8_scales[0, 4 * q : 4 * q + 4, :].bitcast(I32).rearrange("r (g n) -> g r n", g=4),
-            )
+        store_h(A4, 2, 4, 0)
         round_h(vec, A4, 0, 0, P)
         smooth(2)
         store_h(A4, 0, 2, 1)
         round_h(vec, A4, 0, P, HALF)
         smooth(3)
-        store_h(A4, 2, 4, None)
+        store_h(A4, 2, 4, 1)
         quantize_h(A4, 0)
         smooth(4)
         nc.vector.transpose(out=b_cols[:], in_=b_rows[:])

@@ -78,9 +78,6 @@ def tile_mix_save_silu_mix_gelu_kernel(
 
         nc.vector.memset(ws_raw[:].bitcast(I32), 0)
         nc.vector.memset(zero_in[:], 0.0)
-        nc.vector.memset(b_rows[:], 0.0)
-        nc.vector.memset(v4_scale[:].bitcast(I32), 0)
-        nc.vector.memset(v8_scale[:].bitcast(I32), 0)
         nc.vector.memset(warm_bf[:].bitcast(I32), 0)
         nc.scalar.activation(out=zero[:], in_=zero_in[:], func=ACT.Silu)
 
@@ -104,17 +101,6 @@ def tile_mix_save_silu_mix_gelu_kernel(
         nc.sync.dma_start(out=x0_raw[:, 2:4, :], in_=x_rows[0][:, 2:4, :])
         for h in range(2):
             nc.sync.dma_start(out=x1_raw[h][:], in_=x_rows[1][:, :, half(h)])
-        load_w(A8)
-        nc.sync.dma_start(out=sm_sb[:, :, 0:PACK], in_=sm.rearrange("(a p j) -> p a j", a=2, j=PACK))
-        for q in range(QUADS):
-            nc.sync.dma_start(
-                out=v8_scale[SQ * q : SQ * q + 16, :].bitcast(I32),
-                in_=v8_scales[0, 4 * q : 4 * q + 4, :].bitcast(I32).rearrange("r (g n) -> g r n", g=4),
-            )
-        nc.sync.dma_start(out=v8_sb[:].bitcast(I32), in_=v8_words[0].rearrange("p n i -> p (n i)").bitcast(I32))
-        nc.sync.dma_start(out=v4_sb[:].bitcast(I32), in_=v4_words[0].bitcast(I32))
-        nc.sync.dma_start(out=b_rows[0:P:PACK, :], in_=b.rearrange("(c q i) -> q c i", q=QUADS, i=SQ))
-        load_scale_rows(v4_scale[:], v4_scales)
 
         def deal_words(a, lo, hi):
             nc.vector.tensor_copy(
@@ -149,6 +135,20 @@ def tile_mix_save_silu_mix_gelu_kernel(
 
         vec = nc.vector.tensor_copy
         deal_words(A4, 0, 2)
+        nc.vector.memset(b_rows[:], 0.0)
+        nc.vector.memset(v4_scale[:].bitcast(I32), 0)
+        nc.vector.memset(v8_scale[:].bitcast(I32), 0)
+        load_w(A8)
+        nc.sync.dma_start(out=sm_sb[:, :, 0:PACK], in_=sm.rearrange("(a p j) -> p a j", a=2, j=PACK))
+        for q in range(QUADS):
+            nc.sync.dma_start(
+                out=v8_scale[SQ * q : SQ * q + 16, :].bitcast(I32),
+                in_=v8_scales[0, 4 * q : 4 * q + 4, :].bitcast(I32).rearrange("r (g n) -> g r n", g=4),
+            )
+        nc.sync.dma_start(out=v8_sb[:].bitcast(I32), in_=v8_words[0].rearrange("p n i -> p (n i)").bitcast(I32))
+        nc.sync.dma_start(out=v4_sb[:].bitcast(I32), in_=v4_words[0].bitcast(I32))
+        nc.sync.dma_start(out=b_rows[0:P:PACK, :], in_=b.rearrange("(c q i) -> q c i", q=QUADS, i=SQ))
+        load_scale_rows(v4_scale[:], v4_scales)
         quantize(warm_words[:], warm_scale[:], warm_bf[:])
         warm_acc = ps.tile([P, T], F32, name="warm_acc", tag="bank%d" % (TILES - 1))
         for i in range(WARM):

@@ -26,6 +26,7 @@ TILES = N // P
 RUN = 4
 SHARE = 160
 EARLY = 6
+LATE_SCALE_ROWS = {3: 2, 5: 3}
 X_SPLIT = 160
 WARM = 3
 A4, A8 = 1, 0
@@ -231,6 +232,14 @@ def tile_mix_save_silu_mix_gelu_kernel(
         def store_words(a):
             nc.sync.dma_start(out=out_2[a].rearrange("p t i -> p (t i)").bitcast(I32), in_=h_words[a][:].bitcast(I32))
 
+        def store_scale_rows(lo, hi):
+            rows = out_3.rearrange("a (q r) t -> r q a t", r=4)
+            for r in range(lo, hi):
+                nc.sync.dma_start(
+                    out=rows[r].bitcast(I32),
+                    in_=h_scale[r:P:SQ, :].bitcast(I32).rearrange("q (a t) -> q a t", a=2),
+                )
+
         for g, k in ((0, 0), (1, 0), (2, 0), (0, 1), (1, 1), (3, 0), (2, 1), (3, 1)):
             pass1(g, k)
         silu(0)
@@ -268,12 +277,7 @@ def tile_mix_save_silu_mix_gelu_kernel(
         quantize_h(A8, 0)
         quantize_h(A8, 1)
         store_words(A8)
-        rows = out_3.rearrange("a (q r) t -> r q a t", r=4)
-        for r in range(4):
-            nc.sync.dma_start(
-                out=rows[r].bitcast(I32),
-                in_=h_scale[r:P:SQ, :].bitcast(I32).rearrange("q (a t) -> q a t", a=2),
-            )
+        store_scale_rows(0, 2)
 
         first = [ps.tile([P, T], F32, name="first%d" % h, tag="bank%d" % h) for h in range(2)]
         acc2 = {c: ps.tile([P, T], F32, name="acc2_%d" % c, tag="bank%d" % (c + 1)) for c in range(1, TILES - 1)}
@@ -331,3 +335,5 @@ def tile_mix_save_silu_mix_gelu_kernel(
         for c in range(1, TILES):
             gelu(c, whole)
             store_y(c)
+            if c in LATE_SCALE_ROWS:
+                store_scale_rows(LATE_SCALE_ROWS[c], LATE_SCALE_ROWS[c] + 1)

@@ -24,8 +24,8 @@ QUADS = 4
 SQ = 32
 TILES = N // P
 RUN = 4
-SHARE = 160
-EARLY = 6
+SHARE = 128
+EARLY = 4
 LATE_SCALE_ROWS = {3: 2, 5: 3}
 X_SPLIT = 160
 WARM = 3
@@ -109,10 +109,10 @@ def tile_mix_save_silu_mix_gelu_kernel(
                 in_=w_raw[a][:, lo:hi, :].bitcast(U16).rearrange("p k (m j) -> p k j m", j=PACK),
             )
 
-        def deal_scales(a):
-            cols = ws_raw[:].rearrange("p (k n) -> p k n", k=2)[:, :, a * PASS : (a + 1) * PASS]
+        def deal_scales(a, lo, hi):
+            cols = ws_raw[:].rearrange("p (k n) -> p k n", k=2)[:, lo:hi, a * PASS : (a + 1) * PASS]
             nc.vector.tensor_copy(
-                out=w_scale[a][:].rearrange("p (k j m) -> p k j m", k=2, j=PACK),
+                out=w_scale[a][:].rearrange("p (k j m) -> p k j m", k=2, j=PACK)[:, lo:hi],
                 in_=cols.rearrange("p k (m j) -> p k j m", j=PACK),
             )
 
@@ -151,19 +151,20 @@ def tile_mix_save_silu_mix_gelu_kernel(
         nc.sync.dma_start(out=b_rows[0:P:PACK, :], in_=b.rearrange("(c q i) -> q c i", q=QUADS, i=SQ))
         load_scale_rows(v4_scale[:], v4_scales)
         quantize(warm_words[:], warm_scale[:], warm_bf[:])
+        deal_scales(A4, 0, 1)
         warm_acc = ps.tile([P, T], F32, name="warm_acc", tag="bank%d" % (TILES - 1))
         for i in range(WARM):
             nc.tensor.matmul_mx(
                 out=warm_acc[:],
-                lhsT=warm_words[:, 0:P].bitcast(FP8X4),
-                lhsT_scale=warm_scale[:, 0:P],
+                lhsT=w_words[A4][:, 0 : 2 * P].bitcast(FP4X4),
+                lhsT_scale=w_scale[A4][:, 0:P],
                 rhs=warm_words[:].bitcast(FP8X4),
                 rhs_scale=warm_scale[:],
                 start=True,
                 stop=True,
             )
-        deal_scales(A4)
-        deal_scales(A8)
+        deal_scales(A4, 1, 2)
+        deal_scales(A8, 0, 2)
         for h in range(2):
             round_x0(nc.scalar.copy, h * HALF + P, (h + 1) * HALF)
             round_x0(vec, h * HALF, h * HALF + P)
@@ -240,8 +241,10 @@ def tile_mix_save_silu_mix_gelu_kernel(
                     in_=h_scale[r:P:SQ, :].bitcast(I32).rearrange("q (a t) -> q a t", a=2),
                 )
 
-        for g, k in ((0, 0), (1, 0), (2, 0), (0, 1), (1, 1), (3, 0), (2, 1), (3, 1)):
-            pass1(g, k)
+        for h in range(2):
+            for k in range(2):
+                for g in (2 * h, 2 * h + 1):
+                    pass1(g, k)
         silu(0)
         smooth(0)
         store_h(A4, 0, 2, 0)

@@ -58,9 +58,9 @@ def tile_mix_save_silu_mix_gelu_kernel(
         b_cols = tile("b_cols", [P, SQ], F32)
         zero_in = tile("zero_in", [P, 1], F32)
         zero = tile("zero", [P, 1], F32)
-        warm_bf = tile("warm_bf", [P, T * PACK], BF16)
-        warm_words = tile("warm_words", [P, T], U32)
-        warm_scale = tile("warm_scale", [P, T], U8)
+        warm_bf = tile("warm_bf", [P, P * PACK], BF16)
+        warm_words = tile("warm_words", [P, P], U32)
+        warm_scale = tile("warm_scale", [P, P], U8)
         v8_sb = tile("v8_sb", [P, 4 * N], U8)
         v4_sb = tile("v4_sb", [P, 2 * N], U8)
         v4_scale = tile("v4_scale", [P, N], U8)
@@ -156,10 +156,10 @@ def tile_mix_save_silu_mix_gelu_kernel(
         for i in range(WARM):
             nc.tensor.matmul_mx(
                 out=warm_acc[:],
-                lhsT=w_words[A4][:, 0 : 2 * P].bitcast(FP4X4),
-                lhsT_scale=w_scale[A4][:, 0:P],
-                rhs=warm_words[:].bitcast(FP8X4),
-                rhs_scale=warm_scale[:],
+                lhsT=warm_words[:].bitcast(FP8X4),
+                lhsT_scale=warm_scale[:],
+                rhs=w_words[A4][:, 0 : 2 * T].bitcast(FP4X4),
+                rhs_scale=w_scale[A4][:, 0:T],
                 start=True,
                 stop=True,
             )

from contextlib import ExitStack

import concourse.mybir as mybir

K, R, N, T = 1024, 1024, 1024, 512
FLOPS = 2 * K * R * T + 2 * R * N * T

F32 = mybir.dt.float32
BF16 = mybir.dt.bfloat16
I32 = mybir.dt.int32
U32 = mybir.dt.uint32
U16 = mybir.dt.uint16
U8 = mybir.dt.uint8
FP8X4 = mybir.dt.float8_e4m3fn_x4
FP4X4 = mybir.dt.float4_e2m1fn_x4
ACT = mybir.ActivationFunctionType
ALU = mybir.AluOpType

P = 128
PACK = 4
PASS = P * PACK
HALF = T // 2
QUADS = 4
SQ = 32
TILES = N // P
RUN = 4
SHARE = 128
EARLY = 4
LATE_SCALE_ROWS = {3: 2, 5: 3}
X_SPLIT = 160
WARM = 3
A4, A8 = 1, 0


def tile_mix_save_silu_mix_gelu_kernel(
    tc, x, w4_words, w4_scales, sm, v8_words, v8_scales, v4_words, v4_scales, b, out_0, out_1, out_2, out_3
):
    nc = tc.nc
    with ExitStack() as ctx:
        sb = ctx.enter_context(tc.tile_pool(name="sb", bufs=1))
        ps = ctx.enter_context(tc.psum_pool(name="ps", bufs=1))
        ctx.enter_context(tc.manual_schedule())

        def tile(name, shape, dtype):
            return sb.tile(shape, dtype, name=name, align_bytes=64)

        w_raw = [tile("w_raw%d" % a, [P, 2, 2 * PASS], U8) for a in range(2)]
        w_words = [tile("w_words%d" % a, [P, 2 * PACK * 2 * P], U8) for a in range(2)]
        ws_raw = tile("ws_raw", [P, 2 * R], U8)
        w_scale = [tile("w_scale%d" % a, [P, 2 * PACK * P], U8) for a in range(2)]
        x0_raw = tile("x0_raw", [P, PACK, T], F32)
        x1_raw = [tile("x1_raw%d" % h, [P, PACK, HALF], F32) for h in range(2)]
        x_bf = [tile("x_bf%d" % k, [P, T * PACK], BF16) for k in range(2)]
        x_words = [tile("x_words%d" % k, [P, T], U32) for k in range(2)]
        x_scale = [tile("x_scale%d" % k, [P, T], U8) for k in range(2)]
        sm_sb = tile("sm_sb", [P, 2, 2 * PACK], F32)
        b_rows = tile("b_rows", [P, SQ], F32)
        b_cols = tile("b_cols", [P, SQ], F32)
        zero_in = tile("zero_in", [P, 1], F32)
        zero = tile("zero", [P, 1], F32)
        warm_bf = tile("warm_bf", [P, P * PACK], BF16)
        warm_words = tile("warm_words", [P, P], U32)
        warm_scale = tile("warm_scale", [P, P], U8)
        v8_sb = tile("v8_sb", [P, 4 * N], U8)
        v4_sb = tile("v4_sb", [P, 2 * N], U8)
        v4_scale = tile("v4_scale", [P, N], U8)
        v8_scale = tile("v8_scale", [P, N // 4], U8)
        s_sb = [tile("s%d" % g, [P, T], F32) for g in range(TILES)]
        h_sb = [tile("h%d" % a, [P, PACK, T], F32) for a in range(2)]
        h_bf = [[tile("hb%d_%d" % (a, h), [P, HALF * PACK], BF16) for h in range(2)] for a in range(2)]
        h_words = [tile("h_words%d" % a, [P, T], U32) for a in range(2)]
        h_scale = tile("h_scale", [P, 2 * T], U8)
        y_sb = [tile("y%d" % c, [P, T], F32) for c in range(TILES)]

        def half(h):
            return slice(h * HALF, (h + 1) * HALF)

        whole = slice(0, T)

        nc.vector.memset(ws_raw[:].bitcast(I32), 0)
        nc.vector.memset(zero_in[:], 0.0)
        nc.vector.memset(warm_bf[:].bitcast(I32), 0)
        nc.scalar.activation(out=zero[:], in_=zero_in[:], func=ACT.Silu)

        def load_w(a):
            src = w4_words[:, :, a * 2 * PASS : (a + 1) * 2 * PASS].rearrange("k p n -> p k n")
            nc.sync.dma_start(out=w_raw[a][:].bitcast(I32), in_=src.bitcast(I32))

        def load_scale_rows(dst, src):
            passes = src.shape[0]
            rows = src.rearrange("k (q r) n -> r q k n", r=4)
            for r in range(4):
                nc.sync.dma_start(
                    out=dst[r:P:SQ, :].bitcast(I32).rearrange("q (k n) -> q k n", k=passes),
                    in_=rows[r].bitcast(I32),
                )

        x_rows = x.rearrange("(k p j) t -> k p j t", k=2, j=PACK)
        load_w(A4)
        nc.sync.dma_start(out=x0_raw[:, 0:2, :], in_=x_rows[0][:, 0:2, :])
        load_scale_rows(ws_raw[:], w4_scales)
        nc.sync.dma_start(out=x0_raw[:, 2:4, :], in_=x_rows[0][:, 2:4, :])
        for h in range(2):
            nc.sync.dma_start(out=x1_raw[h][:], in_=x_rows[1][:, :, half(h)])

        def deal_words(a, lo, hi):
            nc.vector.tensor_copy(
                out=w_words[a][:].bitcast(U16).rearrange("p (k j m) -> p k j m", k=2, j=PACK)[:, lo:hi],
                in_=w_raw[a][:, lo:hi, :].bitcast(U16).rearrange("p k (m j) -> p k j m", j=PACK),
            )

        def deal_scales(a, lo, hi):
            cols = ws_raw[:].rearrange("p (k n) -> p k n", k=2)[:, lo:hi, a * PASS : (a + 1) * PASS]
            nc.vector.tensor_copy(
                out=w_scale[a][:].rearrange("p (k j m) -> p k j m", k=2, j=PACK)[:, lo:hi],
                in_=cols.rearrange("p k (m j) -> p k j m", j=PACK),
            )

        def interleave(copy, dst, src):
            copy(
                out=dst.rearrange("p (c i j) -> p c j i", i=RUN, j=PACK),
                in_=src.rearrange("p j (c i) -> p c j i", i=RUN),
            )

        def round_x0(copy, lo, hi):
            interleave(copy, x_bf[0][:, lo * PACK : hi * PACK], x0_raw[:, :, lo:hi])

        def round_x1(copy, h, lo, hi):
            interleave(copy, x_bf[1][:, (h * HALF + lo) * PACK : (h * HALF + hi) * PACK], x1_raw[h][:, :, lo:hi])

        def quantize(words, scale, src):
            nc.vector.quantize_mx(out=words.bitcast(FP8X4), scales=scale, in_=src)

        def quantize_x(k, h):
            quantize(x_words[k][:, half(h)], x_scale[k][:, half(h)], x_bf[k][:, h * HALF * PACK : (h + 1) * HALF * PACK])

        vec = nc.vector.tensor_copy
        deal_words(A4, 0, 2)
        nc.vector.memset(b_rows[:], 0.0)
        nc.vector.memset(v4_scale[:].bitcast(I32), 0)
        nc.vector.memset(v8_scale[:].bitcast(I32), 0)
        load_w(A8)
        nc.sync.dma_start(out=sm_sb[:, :, 0:PACK], in_=sm.rearrange("(a p j) -> p a j", a=2, j=PACK))
        for q in range(QUADS):
            nc.sync.dma_start(
                out=v8_scale[SQ * q : SQ * q + 16, :].bitcast(I32),
                in_=v8_scales[0, 4 * q : 4 * q + 4, :].bitcast(I32).rearrange("r (g n) -> g r n", g=4),
            )
        nc.sync.dma_start(out=v8_sb[:].bitcast(I32), in_=v8_words[0].rearrange("p n i -> p (n i)").bitcast(I32))
        nc.sync.dma_start(out=v4_sb[:].bitcast(I32), in_=v4_words[0].bitcast(I32))
        nc.sync.dma_start(out=b_rows[0:P:PACK, :], in_=b.rearrange("(c q i) -> q c i", q=QUADS, i=SQ))
        load_scale_rows(v4_scale[:], v4_scales)
        quantize(warm_words[:], warm_scale[:], warm_bf[:])
        deal_scales(A4, 0, 1)
        warm_acc = ps.tile([P, T], F32, name="warm_acc", tag="bank%d" % (TILES - 1))
        for i in range(WARM):
            nc.tensor.matmul_mx(
                out=warm_acc[:],
                lhsT=warm_words[:].bitcast(FP8X4),
                lhsT_scale=warm_scale[:],
                rhs=w_words[A4][:, 0 : 2 * T].bitcast(FP4X4),
                rhs_scale=w_scale[A4][:, 0:T],
                start=True,
                stop=True,
            )
        deal_scales(A4, 1, 2)
        deal_scales(A8, 0, 2)
        for h in range(2):
            round_x0(nc.scalar.copy, h * HALF + P, (h + 1) * HALF)
            round_x0(vec, h * HALF, h * HALF + P)
        quantize_x(0, 0)
        for h in range(2):
            round_x1(nc.scalar.copy, h, X_SPLIT, HALF)
        round_x1(vec, 0, 0, X_SPLIT)
        quantize_x(0, 1)
        quantize_x(1, 0)
        round_x1(vec, 1, 0, X_SPLIT)
        quantize_x(1, 1)
        deal_words(A8, 0, 1)

        groups = [(A4, (0, 1), 0), (A4, (2, 3), 0), (A4, (0, 1), 1), (A4, (2, 3), 1)]
        groups = groups + [(A8, (0,), None), (A8, (1,), None), (A8, (2, 3), 0), (A8, (2, 3), 1)]
        acc1 = [ps.tile([P, T], F32, name="acc1_%d" % g, tag="bank%d" % g) for g in range(TILES)]

        def pass1(g, k):
            a, rows, h = groups[g]
            cols = whole if h is None else half(h)
            width = T // len(rows)
            for i, j in enumerate(rows):
                c = k * PACK + j
                nc.tensor.matmul_mx(
                    out=acc1[g][:, i * width : (i + 1) * width],
                    lhsT=w_words[a][:, c * 2 * P : (c + 1) * 2 * P].bitcast(FP4X4),
                    lhsT_scale=w_scale[a][:, c * P : (c + 1) * P],
                    rhs=x_words[k][:, cols].bitcast(FP8X4),
                    rhs_scale=x_scale[k][:, cols],
                    start=(k == 0 and i == 0),
                    stop=(k == 1 and i == len(rows) - 1),
                )

        def h_rows(a, h):
            return h_sb[a][:] if h is None else h_sb[a][:, :, half(h)]

        def silu(g):
            nc.scalar.activation(out=s_sb[g][:], in_=acc1[g][:], func=ACT.Silu, bias=zero[:])

        def smooth(g):
            a, rows, h = groups[g]
            width = T // len(rows)
            for i, j in enumerate(rows):
                nc.vector.tensor_scalar(
                    out=h_rows(a, h)[:, j, :],
                    in0=s_sb[g][:, i * width : (i + 1) * width],
                    scalar1=sm_sb[:, a, j : j + 1],
                    scalar2=None,
                    op0=ALU.mult,
                )

        def store_h(a, lo, hi, h):
            rows = out_1[a * PASS : (a + 1) * PASS, :].rearrange("(p j) t -> p j t", j=PACK)
            cols = whole if h is None else half(h)
            nc.sync.dma_start(out=rows[:, lo:hi, cols], in_=h_rows(a, h)[:, lo:hi, :])

        def round_h(copy, a, h, lo, hi):
            interleave(copy, h_bf[a][h][:, lo * PACK : hi * PACK], h_rows(a, h)[:, :, lo:hi])

        def h_scale_cols(a, cols):
            return h_scale[:, a * T + cols.start : a * T + cols.stop]

        def quantize_h(a, h):
            quantize(h_words[a][:, half(h)], h_scale_cols(a, half(h)), h_bf[a][h][:])

        def store_words(a):
            nc.sync.dma_start(out=out_2[a].rearrange("p t i -> p (t i)").bitcast(I32), in_=h_words[a][:].bitcast(I32))

        def store_scale_rows(lo, hi):
            rows = out_3.rearrange("a (q r) t -> r q a t", r=4)
            for r in range(lo, hi):
                nc.sync.dma_start(
                    out=rows[r].bitcast(I32),
                    in_=h_scale[r:P:SQ, :].bitcast(I32).rearrange("q (a t) -> q a t", a=2),
                )

        for h in range(2):
            for k in range(2):
                for g in (2 * h, 2 * h + 1):
                    pass1(g, k)
        silu(0)
        smooth(0)
        store_h(A4, 0, 2, 0)
        deal_words(A8, 1, 2)
        for g in range(PACK, TILES):
            for k in range(2):
                pass1(g, k)
        for g in range(1, TILES):
            silu(g)
        smooth(1)
        store_h(A4, 2, 4, 0)
        round_h(vec, A4, 0, 0, P)
        smooth(2)
        store_h(A4, 0, 2, 1)
        round_h(vec, A4, 0, P, HALF)
        smooth(3)
        store_h(A4, 2, 4, 1)
        quantize_h(A4, 0)
        smooth(4)
        nc.vector.transpose(out=b_cols[:], in_=b_rows[:])
        smooth(5)
        store_h(A8, 0, 2, None)
        round_h(vec, A4, 1, 0, P)
        smooth(6)
        round_h(nc.scalar.copy, A8, 0, 0, SHARE)
        round_h(vec, A4, 1, P, HALF)
        smooth(7)
        store_h(A8, 2, 4, None)
        quantize_h(A4, 1)
        store_words(A4)
        round_h(vec, A8, 0, SHARE, HALF)
        round_h(vec, A8, 1, 0, HALF)
        quantize_h(A8, 0)
        quantize_h(A8, 1)
        store_words(A8)
        store_scale_rows(0, 2)

        first = [ps.tile([P, T], F32, name="first%d" % h, tag="bank%d" % h) for h in range(2)]
        acc2 = {c: ps.tile([P, T], F32, name="acc2_%d" % c, tag="bank%d" % (c + 1)) for c in range(1, TILES - 1)}

        def bank(c, cols):
            return first[cols.start // HALF] if c == 0 else acc2[c]

        def pass_v4(c, cols):
            nc.tensor.matmul_mx(
                out=bank(c, cols)[:, cols],
                lhsT=v4_sb[:, c * 2 * P : (c + 1) * 2 * P].bitcast(FP4X4),
                lhsT_scale=v4_scale[:, c * P : (c + 1) * P],
                rhs=h_words[A4][:, cols].bitcast(FP8X4),
                rhs_scale=h_scale_cols(A4, cols),
                start=(c == 0 or cols.start == 0),
                stop=False,
            )

        def pass_v8(c, cols):
            nc.tensor.matmul_mx(
                out=bank(c, cols)[:, cols],
                lhsT=v8_sb[:, c * 4 * P : (c + 1) * 4 * P].bitcast(FP8X4),
                lhsT_scale=v8_scale[4 * (c // 2) : P, (c % 2) * P : (c % 2 + 1) * P],
                rhs=h_words[A8][:, cols].bitcast(FP8X4),
                rhs_scale=h_scale_cols(A8, cols),
                start=False,
                stop=(c == 0 or cols.stop == T),
            )

        def gelu(c, cols):
            nc.scalar.activation(
                out=y_sb[c][:, cols], in_=bank(c, cols)[:, cols], func=ACT.Gelu_apprx_tanh, bias=b_cols[:, c * PACK : c * PACK + 1]
            )

        def store_y(c):
            nc.sync.dma_start(out=out_0[c * P : (c + 1) * P, :], in_=y_sb[c][:])

        for c in range(TILES - 1):
            pass_v4(c, half(0))
        for c in range(EARLY):
            pass_v4(c, half(1))
        for h in range(2):
            for c in range(2):
                pass_v8(c, half(h))
        for h in range(2):
            gelu(0, half(h))
        store_y(0)
        acc2[TILES - 1] = ps.tile([P, T], F32, name="acc2_last", tag="bank0")
        for c in range(2, TILES):
            if c == TILES - 1:
                pass_v4(c, whole)
            elif c >= EARLY:
                pass_v4(c, half(1))
            pass_v8(c, whole)
        for c in range(1, TILES):
            gelu(c, whole)
            store_y(c)
            if c in LATE_SCALE_ROWS:
                store_scale_rows(LATE_SCALE_ROWS[c], LATE_SCALE_ROWS[c] + 1)
